import numpy as np
import ml_dtypes


def mxq(x, axis, fmt="e4m3"):
    dtype, down = {"e4m3": (ml_dtypes.float8_e4m3fn, 7), "e5m2": (ml_dtypes.float8_e5m2, 14)}[fmt]
    v = np.moveaxis(np.asarray(x, np.float32).astype(ml_dtypes.bfloat16).astype(np.float64), axis, -1)
    blocks = v.reshape(v.shape[:-1] + (-1, 32))
    amax = np.abs(blocks).max(-1, keepdims=True)
    byte = np.maximum(np.where(amax > 0, np.frexp(amax)[1] - 1 + 127, 0) - down, 1)
    scale = np.exp2(byte - 127.0)
    codes = (blocks / scale).astype(np.float32).astype(dtype).astype(np.float64)
    return np.moveaxis((codes * scale).reshape(v.shape), -1, axis)


WIDE = False


def mx_kscale(k):
    if not WIDE:
        return np.ones(k)
    levels = np.array([10, -10, 5, -5, 0])
    if k % 512:
        return np.exp2(np.random.permutation(np.resize(levels, k // 32))).repeat(32)
    a = np.empty((k // 512, 16))
    for p in range(k // 512):
        a[p, :8] = np.random.permutation(np.resize(levels, 8))
        for g in range(8):
            far = levels[np.abs(levels - a[p, g]) >= 10]
            a[p, g + 8] = far[np.random.randint(len(far))]
    return np.exp2(a.ravel()).repeat(32)


def f64(x):
    return np.asarray(x).astype(np.float64)


def striped(idx):
    return np.tile(idx.reshape(-1, 16).T, (8, 1)).astype(np.uint16)


def unstriped(offs):
    return offs[:16].T.reshape(-1).astype(np.int64)


def striped8(idx):
    return np.concatenate([x.reshape(-1, 16).T for x in idx]).astype(np.uint16)


def runs(offs, k):
    lists = np.stack([offs[16 * r : 16 * r + 16].T.reshape(-1) for r in range(8)]).astype(np.int64)
    return lists[np.arange(k) % 512 // 64]


def pack_weight(w):
    k, n = w.shape
    w = f64(np.asarray(w, np.float32).astype(ml_dtypes.bfloat16)).reshape(k // 32, 32, n)
    amax = np.abs(w).max(1)
    byte = np.clip(np.where(amax > 0, np.frexp(amax)[1] - 1 + 127 - 7, 1), 1, 254)
    scaled = (w * np.exp2(127.0 - byte)[:, None, :]).reshape(k, n).astype(np.float32)
    words = np.ascontiguousarray(scaled.reshape(k // 512, 128, 4, n).transpose(0, 1, 3, 2)).astype(ml_dtypes.float8_e4m3fn).view(np.uint8)
    return words, np.ascontiguousarray(byte.astype(np.uint8).reshape(k // 512, 16, n))


def unpack_weight(words, scales):
    g, p, n, _ = words.shape
    vals = np.ascontiguousarray(words).view(ml_dtypes.float8_e4m3fn).astype(np.float64) * np.repeat(np.exp2(scales.astype(np.float64) - 127.0), 8, axis=1)[..., None]
    return vals.transpose(0, 1, 3, 2).reshape(g * 512, n)


K, T, S, N, U = 1024, 2048, 512, 512, 1024


def setup_inputs():
    n = np.random.standard_normal
    s = mx_kscale(K)[:, None]
    packed_xT = pack_weight(n((K, T)) * s)
    return {
        "x_words": packed_xT[0],
        "x_scales": packed_xT[1],
        "w1": (n((K, N)) / np.sqrt(K) / s).astype(np.float32),
        "par": n((N, U)).astype(np.float32),
        "offs": striped(np.random.permutation(T)[:S]),
        "ent": striped8(np.stack([np.random.permutation(U)[:S] for _ in range(8)])),
    }


def reference(x_words, x_scales, w1, par, offs, ent):
    o = f64(par)[np.arange(N)[:, None], runs(ent, N)]
    xq = unpack_weight(x_words, x_scales)[:, unstriped(offs)]
    y = mxq(f64(w1), 0, "e4m3").T @ xq
    pn = 0.875 * o - np.clip(y, -0.75, 0.75)
    out = f64(par).copy()
    out[np.arange(N)[:, None], runs(ent, N)] = pn
    return out

@@ -1,0 +1,114 @@
+from contextlib import ExitStack
+
+import concourse.mybir as mybir
+
+K, T, S, N, U = 1024, 2048, 512, 512, 1024
+FLOPS = 2 * K * N * S
+
+F32 = mybir.dt.float32
+BF16 = mybir.dt.bfloat16
+I32 = mybir.dt.int32
+U32 = mybir.dt.uint32
+U16 = mybir.dt.uint16
+U8 = mybir.dt.uint8
+FP8X4 = mybir.dt.float8_e4m3fn_x4
+ALU = mybir.AluOpType
+COPY = mybir.ActivationFunctionType.Copy
+
+P = 128
+PACK = 4
+K_PASS = P * PACK
+PASSES = K // K_PASS
+TILES = N // P
+QUAD = 32
+DECAY = 0.875
+CLIP = 0.75
+
+
+def tile_picked_clipsgd_none_p_kernel(tc, x_words, x_scales, w1, par, offs, ent, out):
+    nc = tc.nc
+    par_rows = par.rearrange("(p t) u -> p t u", t=TILES)
+    out_rows = out.rearrange("(p t) u -> p t u", t=TILES)
+
+    with ExitStack() as ctx:
+        keep = ctx.enter_context(tc.tile_pool(name="keep", bufs=1))
+        psum = ctx.enter_context(tc.psum_pool(name="psum", bufs=1))
+
+        offs_sb = keep.tile([P, S // 16], U16, name="offs_sb")
+        ent_sb = keep.tile([P, S // 16], U16, name="ent_sb")
+        w_raw = [keep.tile([P, PACK, N], F32, name=f"w_raw{g}") for g in range(PASSES)]
+        x_all = [keep.tile([P, T], U32, name=f"x_all{g}") for g in range(PASSES)]
+        xs_all = keep.tile([P, T], U8, name="xs_all")
+        table = [keep.tile([P, U], F32, name=f"table{t}") for t in range(TILES)]
+
+        def load_w(g):
+            rows = w1[g * K_PASS : (g + 1) * K_PASS, :]
+            nc.sync.dma_start(out=w_raw[g][:], in_=rows.rearrange("(p j) c -> p j c", j=PACK))
+
+        nc.vector.memset(xs_all[:].bitcast(I32), 0)
+        load_w(0)
+        for g in range(PASSES):
+            for i in range(4):
+                nc.sync.dma_start(
+                    out=xs_all[4 * g + i : P : QUAD, :].bitcast(I32),
+                    in_=x_scales[g, i:16:4, :].bitcast(I32),
+                )
+        nc.sync.dma_start(offs_sb[:], offs)
+        load_w(1)
+        nc.sync.dma_start(ent_sb[:], ent)
+        for g in range(PASSES):
+            nc.sync.dma_start(
+                out=x_all[g][:].bitcast(I32),
+                in_=x_words[g].rearrange("p n r -> p (n r)").bitcast(I32),
+            )
+        for t in range(TILES):
+            nc.sync.dma_start(out=table[t][:], in_=par_rows[:, t, :])
+
+        xs = keep.tile([P, S], U8, name="xs", align_bytes=64)
+        nc.vector.tensor_copy(xs[:], xs_all[:].indirect(offs_sb[:]))
+
+        w_bf = [keep.tile([P, TILES, P, PACK], BF16, name=f"w_bf{g}", align_bytes=64) for g in range(PASSES)]
+        w_codes = [keep.tile([P, N], U32, name=f"w_codes{g}", align_bytes=64) for g in range(PASSES)]
+        w_scales = [keep.tile([P, N], U8, name=f"w_scales{g}", align_bytes=64) for g in range(PASSES)]
+        x_codes = [keep.tile([P, S], U32, name=f"x_codes{g}", align_bytes=64) for g in range(PASSES)]
+
+        def dealt(g):
+            return (
+                w_bf[g][:].rearrange("p t m j -> p m j t"),
+                w_raw[g][:].rearrange("p j (m t) -> p m j t", t=TILES),
+            )
+
+        dst, src = dealt(0)
+        nc.scalar.activation(dst, src, COPY)
+        dst, src = dealt(1)
+        nc.vector.tensor_copy(dst, src)
+        for g in range(PASSES):
+            nc.vector.quantize_mx(
+                out=w_codes[g][:].bitcast(FP8X4),
+                scales=w_scales[g][:],
+                in_=w_bf[g][:].rearrange("p t m j -> p (t m j)"),
+            )
+        acc = [psum.tile([P, S], F32, name=f"acc{t}") for t in range(TILES)]
+        for g in range(PASSES):
+            nc.vector.tensor_copy(x_codes[g][:], x_all[g][:].indirect(offs_sb[:]))
+            for t in range(TILES):
+                cols = slice(t * P, (t + 1) * P)
+                nc.tensor.matmul_mx(
+                    out=acc[t][:],
+                    lhsT=w_codes[g][:, cols].bitcast(FP8X4),
+                    lhsT_scale=w_scales[g][:, cols],
+                    rhs=x_codes[g][:].bitcast(FP8X4),
+                    rhs_scale=xs[4 * g : P, :],
+                    start=(g == 0),
+                    stop=(g == PASSES - 1),
+                )
+
+        for t in range(TILES):
+            neg_y = keep.tile([P, S], F32, name=f"neg_y{t}")
+            nc.scalar.activation(neg_y[:], acc[t][:], COPY, scale=-1.0)
+            shrunk = keep.tile([P, S], F32, name=f"shrunk{t}")
+            nc.vector.tensor_scalar(shrunk[:], table[t][:].indirect(ent_sb[:]), DECAY, 0.0, ALU.mult, ALU.add)
+            step = keep.tile([P, S], F32, name=f"step{t}")
+            nc.vector.tensor_scalar(step[:], neg_y[:], -CLIP, CLIP, ALU.max, ALU.min)
+            nc.vector.tensor_tensor(table[t][:].indirect(ent_sb[:]), shrunk[:], step[:], ALU.add)
+            nc.sync.dma_start(out=out_rows[:, t, :], in_=table[t][:])

@@ -23,6 +23,7 @@ TILES = N // P
 QUAD = 32
 DECAY = 0.875
 CLIP = 0.75
+M_VECTOR = 80
 
 
 def tile_picked_clipsgd_none_p_kernel(tc, x_words, x_scales, w1, par, offs, ent, out):
@@ -45,70 +46,86 @@ def tile_picked_clipsgd_none_p_kernel(tc, x_words, x_scales, w1, par, offs, ent,
             rows = w1[g * K_PASS : (g + 1) * K_PASS, :]
             nc.sync.dma_start(out=w_raw[g][:], in_=rows.rearrange("(p j) c -> p j c", j=PACK))
 
-        nc.vector.memset(xs_all[:].bitcast(I32), 0)
-        load_w(0)
-        for g in range(PASSES):
-            for i in range(4):
-                nc.sync.dma_start(
-                    out=xs_all[4 * g + i : P : QUAD, :].bitcast(I32),
-                    in_=x_scales[g, i:16:4, :].bitcast(I32),
-                )
-        nc.sync.dma_start(offs_sb[:], offs)
-        load_w(1)
-        nc.sync.dma_start(ent_sb[:], ent)
-        for g in range(PASSES):
+        def load_x(g):
             nc.sync.dma_start(
                 out=x_all[g][:].bitcast(I32),
                 in_=x_words[g].rearrange("p n r -> p (n r)").bitcast(I32),
             )
-        for t in range(TILES):
+
+        def load_table(t):
             nc.sync.dma_start(out=table[t][:], in_=par_rows[:, t, :])
 
-        xs = keep.tile([P, S], U8, name="xs", align_bytes=64)
-        nc.vector.tensor_copy(xs[:], xs_all[:].indirect(offs_sb[:]))
+        nc.gpsimd.memset(xs_all[:].bitcast(I32), 0)
+        load_w(0)
+        for q in range(P // QUAD):
+            nc.sync.dma_start(
+                out=xs_all[q * QUAD : q * QUAD + 4 * PASSES, :].bitcast(I32),
+                in_=x_scales[:, 4 * q : 4 * q + 4, :].bitcast(I32),
+            )
+        nc.sync.dma_start(offs_sb[:], offs)
+        load_x(0)
+        load_w(1)
+        load_x(1)
+        nc.sync.dma_start(ent_sb[:], ent)
+        for t in range(TILES):
+            load_table(t)
 
+        xs = keep.tile([P, S], U8, name="xs", align_bytes=64)
         w_bf = [keep.tile([P, TILES, P, PACK], BF16, name=f"w_bf{g}", align_bytes=64) for g in range(PASSES)]
         w_codes = [keep.tile([P, N], U32, name=f"w_codes{g}", align_bytes=64) for g in range(PASSES)]
         w_scales = [keep.tile([P, N], U8, name=f"w_scales{g}", align_bytes=64) for g in range(PASSES)]
         x_codes = [keep.tile([P, S], U32, name=f"x_codes{g}", align_bytes=64) for g in range(PASSES)]
 
-        def dealt(g):
-            return (
-                w_bf[g][:].rearrange("p t m j -> p m j t"),
-                w_raw[g][:].rearrange("p j (m t) -> p m j t", t=TILES),
-            )
-
-        dst, src = dealt(0)
-        nc.scalar.activation(dst, src, COPY)
-        dst, src = dealt(1)
-        nc.vector.tensor_copy(dst, src)
         for g in range(PASSES):
+            dst = w_bf[g][:].rearrange("p t m j -> p m j t")
+            src = w_raw[g][:].rearrange("p j (m t) -> p m j t", t=TILES)
+            nc.vector.tensor_copy(dst[:, :M_VECTOR], src[:, :M_VECTOR])
+            nc.scalar.activation(dst[:, M_VECTOR:], src[:, M_VECTOR:], COPY)
+            if g == 0:
+                nc.vector.tensor_copy(xs[:], xs_all[:].indirect(offs_sb[:]))
             nc.vector.quantize_mx(
                 out=w_codes[g][:].bitcast(FP8X4),
                 scales=w_scales[g][:],
                 in_=w_bf[g][:].rearrange("p t m j -> p (t m j)"),
             )
-        acc = [psum.tile([P, S], F32, name=f"acc{t}") for t in range(TILES)]
-        for g in range(PASSES):
-            nc.vector.tensor_copy(x_codes[g][:], x_all[g][:].indirect(offs_sb[:]))
-            for t in range(TILES):
-                cols = slice(t * P, (t + 1) * P)
-                nc.tensor.matmul_mx(
-                    out=acc[t][:],
-                    lhsT=w_codes[g][:, cols].bitcast(FP8X4),
-                    lhsT_scale=w_scales[g][:, cols],
-                    rhs=x_codes[g][:].bitcast(FP8X4),
-                    rhs_scale=xs[4 * g : P, :],
-                    start=(g == 0),
-                    stop=(g == PASSES - 1),
-                )
+            if g == 0:
+                nc.vector.tensor_copy(x_codes[0][:], x_all[0][:].indirect(offs_sb[:]))
+
+        halves = [slice(0, S // 2), slice(S // 2, S)]
+        pieces = [(0, h) for h in halves] + [(t, slice(0, S)) for t in range(1, TILES)]
+        acc = [psum.tile([P, js.stop - js.start], F32, name=f"acc{n}") for n, (t, js) in enumerate(pieces)]
+
+        def columns(js):
+            return slice(js.start // 16, js.stop // 16)
+
+        def product(g, n):
+            t, js = pieces[n]
+            cols = slice(t * P, (t + 1) * P)
+            nc.tensor.matmul_mx(
+                out=acc[n][:],
+                lhsT=w_codes[g][:, cols].bitcast(FP8X4),
+                lhsT_scale=w_scales[g][:, cols],
+                rhs=x_codes[g][:, js].bitcast(FP8X4),
+                rhs_scale=xs[4 * g : P, js],
+                start=(g == 0),
+                stop=(g == PASSES - 1),
+            )
+
+        for n in range(len(pieces)):
+            product(0, n)
+        for js in halves:
+            nc.vector.tensor_copy(x_codes[1][:, js], x_all[1][:].indirect(offs_sb[:, columns(js)]))
+        for n in range(len(pieces)):
+            product(1, n)
 
         for t in range(TILES):
-            neg_y = keep.tile([P, S], F32, name=f"neg_y{t}")
-            nc.scalar.activation(neg_y[:], acc[t][:], COPY, scale=-1.0)
             shrunk = keep.tile([P, S], F32, name=f"shrunk{t}")
             nc.vector.tensor_scalar(shrunk[:], table[t][:].indirect(ent_sb[:]), DECAY, 0.0, ALU.mult, ALU.add)
-            step = keep.tile([P, S], F32, name=f"step{t}")
-            nc.vector.tensor_scalar(step[:], neg_y[:], -CLIP, CLIP, ALU.max, ALU.min)
+            step = keep.tile([P, S], F32, name="step")
+            for n, (tile, js) in enumerate(pieces):
+                if tile == t:
+                    neg_y = keep.tile([P, js.stop - js.start], F32, name=f"neg_y{n}")
+                    nc.scalar.activation(neg_y[:], acc[n][:], COPY, scale=-1.0)
+                    nc.gpsimd.tensor_scalar(step[:, js], neg_y[:], CLIP, -CLIP, ALU.min, ALU.max)
             nc.vector.tensor_tensor(table[t][:].indirect(ent_sb[:]), shrunk[:], step[:], ALU.add)
             nc.sync.dma_start(out=out_rows[:, t, :], in_=table[t][:])

@@ -52,22 +52,29 @@ def tile_picked_clipsgd_none_p_kernel(tc, x_words, x_scales, w1, par, offs, ent,
                 in_=x_words[g].rearrange("p n r -> p (n r)").bitcast(I32),
             )
 
+        def load_scales(rows):
+            for r in rows:
+                g, i = divmod(r, 4)
+                nc.sync.dma_start(
+                    out=xs_all[r:P:QUAD, :].bitcast(I32),
+                    in_=x_scales[g, i:16:4, :].bitcast(I32),
+                )
+
         def load_table(t):
             nc.sync.dma_start(out=table[t][:], in_=par_rows[:, t, :])
 
+        scale_rows = [4 * g + i for i in range(4) for g in range(PASSES)]
         nc.gpsimd.memset(xs_all[:].bitcast(I32), 0)
         load_w(0)
-        for q in range(P // QUAD):
-            nc.sync.dma_start(
-                out=xs_all[q * QUAD : q * QUAD + 4 * PASSES, :].bitcast(I32),
-                in_=x_scales[:, 4 * q : 4 * q + 4, :].bitcast(I32),
-            )
+        load_scales(scale_rows[:5])
         nc.sync.dma_start(offs_sb[:], offs)
         load_x(0)
+        load_scales(scale_rows[5:])
         load_w(1)
-        load_x(1)
         nc.sync.dma_start(ent_sb[:], ent)
-        for t in range(TILES):
+        load_table(0)
+        load_x(1)
+        for t in range(1, TILES):
             load_table(t)
 
         xs = keep.tile([P, S], U8, name="xs", align_bytes=64)
@@ -81,8 +88,6 @@ def tile_picked_clipsgd_none_p_kernel(tc, x_words, x_scales, w1, par, offs, ent,
             src = w_raw[g][:].rearrange("p j (m t) -> p m j t", t=TILES)
             nc.vector.tensor_copy(dst[:, :M_VECTOR], src[:, :M_VECTOR])
             nc.scalar.activation(dst[:, M_VECTOR:], src[:, M_VECTOR:], COPY)
-            if g == 0:
-                nc.vector.tensor_copy(xs[:], xs_all[:].indirect(offs_sb[:]))
             nc.vector.quantize_mx(
                 out=w_codes[g][:].bitcast(FP8X4),
                 scales=w_scales[g][:],
@@ -90,6 +95,7 @@ def tile_picked_clipsgd_none_p_kernel(tc, x_words, x_scales, w1, par, offs, ent,
             )
             if g == 0:
                 nc.vector.tensor_copy(x_codes[0][:], x_all[0][:].indirect(offs_sb[:]))
+                nc.vector.tensor_copy(xs[:], xs_all[:].indirect(offs_sb[:]))
 
         halves = [slice(0, S // 2), slice(S // 2, S)]
         pieces = [(0, h) for h in halves] + [(t, slice(0, S)) for t in range(1, TILES)]
@@ -113,19 +119,25 @@ def tile_picked_clipsgd_none_p_kernel(tc, x_words, x_scales, w1, par, offs, ent,
 
         for n in range(len(pieces)):
             product(0, n)
+        shrunk = [keep.tile([P, S], F32, name=f"shrunk{t}", tag=f"shrunk{t}") for t in range(TILES)]
+
+        def shrink(t):
+            nc.vector.tensor_scalar(shrunk[t][:], table[t][:].indirect(ent_sb[:]), DECAY, 0.0, ALU.mult, ALU.add)
+
+        shrink(0)
         for js in halves:
             nc.vector.tensor_copy(x_codes[1][:, js], x_all[1][:].indirect(offs_sb[:, columns(js)]))
         for n in range(len(pieces)):
             product(1, n)
 
         for t in range(TILES):
-            shrunk = keep.tile([P, S], F32, name=f"shrunk{t}")
-            nc.vector.tensor_scalar(shrunk[:], table[t][:].indirect(ent_sb[:]), DECAY, 0.0, ALU.mult, ALU.add)
-            step = keep.tile([P, S], F32, name="step")
+            if t + 1 < TILES:
+                shrink(t + 1)
+            step = keep.tile([P, S], F32, name=f"step{t}", tag="shrunk0" if t == 2 else "step")
             for n, (tile, js) in enumerate(pieces):
                 if tile == t:
                     neg_y = keep.tile([P, js.stop - js.start], F32, name=f"neg_y{n}")
                     nc.scalar.activation(neg_y[:], acc[n][:], COPY, scale=-1.0)
                     nc.gpsimd.tensor_scalar(step[:, js], neg_y[:], CLIP, -CLIP, ALU.min, ALU.max)
-            nc.vector.tensor_tensor(table[t][:].indirect(ent_sb[:]), shrunk[:], step[:], ALU.add)
+            nc.vector.tensor_tensor(table[t][:].indirect(ent_sb[:]), shrunk[t][:], step[:], ALU.add)
             nc.sync.dma_start(out=out_rows[:, t, :], in_=table[t][:])

@@ -21,9 +21,13 @@ K_PASS = P * PACK
 PASSES = K // K_PASS
 TILES = N // P
 QUAD = 32
+QUAD_ROWS = 4
+GROUP = 16
+PAIR = 2 * S
 DECAY = 0.875
 CLIP = 0.75
 M_VECTOR = 80
+SCALE_LOADS_FIRST = 5
 
 
 def tile_picked_clipsgd_none_p_kernel(tc, x_words, x_scales, w1, par, offs, ent, out):
@@ -35,8 +39,8 @@ def tile_picked_clipsgd_none_p_kernel(tc, x_words, x_scales, w1, par, offs, ent,
         keep = ctx.enter_context(tc.tile_pool(name="keep", bufs=1))
         psum = ctx.enter_context(tc.psum_pool(name="psum", bufs=1))
 
-        offs_sb = keep.tile([P, S // 16], U16, name="offs_sb")
-        ent_sb = keep.tile([P, S // 16], U16, name="ent_sb")
+        offs_sb = keep.tile([P, S // GROUP], U16, name="offs_sb")
+        ent_sb = keep.tile([P, S // GROUP], U16, name="ent_sb")
         w_raw = [keep.tile([P, PACK, N], F32, name=f"w_raw{g}") for g in range(PASSES)]
         x_all = [keep.tile([P, T], U32, name=f"x_all{g}") for g in range(PASSES)]
         xs_all = keep.tile([P, T], U8, name="xs_all")
@@ -52,24 +56,24 @@ def tile_picked_clipsgd_none_p_kernel(tc, x_words, x_scales, w1, par, offs, ent,
                 in_=x_words[g].rearrange("p n r -> p (n r)").bitcast(I32),
             )
 
-        def load_scales(rows):
-            for r in rows:
-                g, i = divmod(r, 4)
+        def load_scales(loads):
+            for g, i in loads:
                 nc.sync.dma_start(
-                    out=xs_all[r:P:QUAD, :].bitcast(I32),
-                    in_=x_scales[g, i:16:4, :].bitcast(I32),
+                    out=xs_all[QUAD_ROWS * g + i : P : QUAD, :].bitcast(I32),
+                    in_=x_scales[g, i : QUAD_ROWS * (P // QUAD) : QUAD_ROWS, :].bitcast(I32),
                 )
 
         def load_table(t):
             nc.sync.dma_start(out=table[t][:], in_=par_rows[:, t, :])
 
-        scale_rows = [4 * g + i for i in range(4) for g in range(PASSES)]
+        scale_loads = [(g, i) for i in range(QUAD_ROWS) for g in range(PASSES)]
         nc.gpsimd.memset(xs_all[:].bitcast(I32), 0)
+
         load_w(0)
-        load_scales(scale_rows[:5])
+        load_scales(scale_loads[:SCALE_LOADS_FIRST])
         nc.sync.dma_start(offs_sb[:], offs)
         load_x(0)
-        load_scales(scale_rows[5:])
+        load_scales(scale_loads[SCALE_LOADS_FIRST:])
         load_w(1)
         nc.sync.dma_start(ent_sb[:], ent)
         load_table(0)
@@ -77,7 +81,7 @@ def tile_picked_clipsgd_none_p_kernel(tc, x_words, x_scales, w1, par, offs, ent,
         for t in range(1, TILES):
             load_table(t)
 
-        xs = keep.tile([P, S], U8, name="xs", align_bytes=64)
+        x_scale = keep.tile([P, S], U8, name="x_scale", align_bytes=64)
         w_bf = [keep.tile([P, TILES, P, PACK], BF16, name=f"w_bf{g}", align_bytes=64) for g in range(PASSES)]
         w_codes = [keep.tile([P, N], U32, name=f"w_codes{g}", align_bytes=64) for g in range(PASSES)]
         w_scales = [keep.tile([P, N], U8, name=f"w_scales{g}", align_bytes=64) for g in range(PASSES)]
@@ -95,30 +99,28 @@ def tile_picked_clipsgd_none_p_kernel(tc, x_words, x_scales, w1, par, offs, ent,
             )
             if g == 0:
                 nc.vector.tensor_copy(x_codes[0][:], x_all[0][:].indirect(offs_sb[:]))
-                nc.vector.tensor_copy(xs[:], xs_all[:].indirect(offs_sb[:]))
+                nc.vector.tensor_copy(x_scale[:], xs_all[:].indirect(offs_sb[:]))
 
         halves = [slice(0, S // 2), slice(S // 2, S)]
-        pieces = [(0, h) for h in halves] + [(t, slice(0, S)) for t in range(1, TILES)]
+        pieces = [(0, js) for js in halves] + [(t, slice(0, S)) for t in range(1, TILES)]
         acc = [psum.tile([P, js.stop - js.start], F32, name=f"acc{n}") for n, (t, js) in enumerate(pieces)]
-
-        def columns(js):
-            return slice(js.start // 16, js.stop // 16)
 
         def product(g, n):
             t, js = pieces[n]
-            cols = slice(t * P, (t + 1) * P)
+            features = slice(t * P, (t + 1) * P)
             nc.tensor.matmul_mx(
                 out=acc[n][:],
-                lhsT=w_codes[g][:, cols].bitcast(FP8X4),
-                lhsT_scale=w_scales[g][:, cols],
+                lhsT=w_codes[g][:, features].bitcast(FP8X4),
+                lhsT_scale=w_scales[g][:, features],
                 rhs=x_codes[g][:, js].bitcast(FP8X4),
-                rhs_scale=xs[4 * g : P, js],
+                rhs_scale=x_scale[QUAD_ROWS * g : P, js],
                 start=(g == 0),
                 stop=(g == PASSES - 1),
             )
 
         for n in range(len(pieces)):
             product(0, n)
+
         shrunk = [keep.tile([P, S], F32, name=f"shrunk{t}", tag=f"shrunk{t}") for t in range(TILES)]
 
         def shrink(t):
@@ -126,18 +128,33 @@ def tile_picked_clipsgd_none_p_kernel(tc, x_words, x_scales, w1, par, offs, ent,
 
         shrink(0)
         for js in halves:
-            nc.vector.tensor_copy(x_codes[1][:, js], x_all[1][:].indirect(offs_sb[:, columns(js)]))
+            list_columns = slice(js.start // GROUP, js.stop // GROUP)
+            nc.vector.tensor_copy(x_codes[1][:, js], x_all[1][:].indirect(offs_sb[:, list_columns]))
         for n in range(len(pieces)):
             product(1, n)
 
-        for t in range(TILES):
-            if t + 1 < TILES:
-                shrink(t + 1)
-            step = keep.tile([P, S], F32, name=f"step{t}", tag="shrunk0" if t == 2 else "step")
-            for n, (tile, js) in enumerate(pieces):
-                if tile == t:
-                    neg_y = keep.tile([P, js.stop - js.start], F32, name=f"neg_y{n}")
-                    nc.scalar.activation(neg_y[:], acc[n][:], COPY, scale=-1.0)
-                    nc.gpsimd.tensor_scalar(step[:, js], neg_y[:], CLIP, -CLIP, ALU.min, ALU.max)
-            nc.vector.tensor_tensor(table[t][:].indirect(ent_sb[:]), shrunk[t][:], step[:], ALU.add)
+        neg_y = keep.tile([P, TILES * S], F32, name="neg_y")
+        for n, (t, js) in enumerate(pieces):
+            nc.scalar.activation(neg_y[:, t * S + js.start : t * S + js.stop], acc[n][:], COPY, scale=-1.0)
+
+        def clip(step, first, last):
+            base = first // PAIR * PAIR
+            nc.gpsimd.tensor_scalar(step[:, first - base : last - base], neg_y[:, first:last], CLIP, -CLIP, ALU.min, ALU.max)
+
+        def scatter(t, step):
+            own = slice(t % 2 * S, (t % 2 + 1) * S)
+            nc.vector.tensor_tensor(table[t][:].indirect(ent_sb[:]), shrunk[t][:], step[:, own], ALU.add)
             nc.sync.dma_start(out=out_rows[:, t, :], in_=table[t][:])
+
+        shrink(1)
+        shrink(2)
+        step_low = keep.tile([P, PAIR], F32, name="step_low")
+        clip(step_low, 0, S // 2)
+        clip(step_low, S // 2, PAIR)
+        scatter(0, step_low)
+        shrink(3)
+        step_high = keep.tile([P, PAIR], F32, name="step_high", tag="shrunk0")
+        clip(step_high, PAIR, 2 * PAIR)
+        scatter(1, step_low)
+        scatter(2, step_high)
+        scatter(3, step_high)

@@ -23,7 +23,6 @@ TILES = N // P
 QUAD = 32
 QUAD_ROWS = 4
 GROUP = 16
-PAIR = 2 * S
 DECAY = 0.875
 CLIP = 0.75
 M_VECTOR = 80
@@ -44,7 +43,7 @@ def tile_picked_clipsgd_none_p_kernel(tc, x_words, x_scales, w1, par, offs, ent,
         w_raw = [keep.tile([P, PACK, N], F32, name=f"w_raw{g}") for g in range(PASSES)]
         x_all = [keep.tile([P, T], U32, name=f"x_all{g}") for g in range(PASSES)]
         xs_all = keep.tile([P, T], U8, name="xs_all")
-        table = [keep.tile([P, U], F32, name=f"table{t}") for t in range(TILES)]
+        table = [keep.tile([P, U + S if t in (0, TILES - 1) else U], F32, name=f"table{t}") for t in range(TILES)]
 
         def load_w(g):
             rows = w1[g * K_PASS : (g + 1) * K_PASS, :]
@@ -64,7 +63,7 @@ def tile_picked_clipsgd_none_p_kernel(tc, x_words, x_scales, w1, par, offs, ent,
                 )
 
         def load_table(t):
-            nc.sync.dma_start(out=table[t][:], in_=par_rows[:, t, :])
+            nc.sync.dma_start(out=table[t][:, :U], in_=par_rows[:, t, :])
 
         scale_loads = [(g, i) for i in range(QUAD_ROWS) for g in range(PASSES)]
         nc.gpsimd.memset(xs_all[:].bitcast(I32), 0)
@@ -121,7 +120,7 @@ def tile_picked_clipsgd_none_p_kernel(tc, x_words, x_scales, w1, par, offs, ent,
         for n in range(len(pieces)):
             product(0, n)
 
-        shrunk = [keep.tile([P, S], F32, name=f"shrunk{t}", tag=f"shrunk{t}") for t in range(TILES)]
+        shrunk = [keep.tile([P, S], F32, name=f"shrunk{t}") for t in range(TILES - 1)] + [table[0][:, U:]]
 
         def shrink(t):
             nc.vector.tensor_scalar(shrunk[t][:], table[t][:].indirect(ent_sb[:]), DECAY, 0.0, ALU.mult, ALU.add)
@@ -133,28 +132,16 @@ def tile_picked_clipsgd_none_p_kernel(tc, x_words, x_scales, w1, par, offs, ent,
         for n in range(len(pieces)):
             product(1, n)
 
-        neg_y = keep.tile([P, TILES * S], F32, name="neg_y")
+        y_sb = keep.tile([P, TILES * S], F32, name="y_sb")
+        step = keep.tile([P, S], F32, name="step")
+        new = [table[TILES - 1][:, U:] if t == 1 else keep.tile([P, S], F32, name=f"new{t}") for t in range(TILES)]
+        for t in range(1, TILES):
+            shrink(t)
         for n, (t, js) in enumerate(pieces):
-            nc.scalar.activation(neg_y[:, t * S + js.start : t * S + js.stop], acc[n][:], COPY, scale=-1.0)
-
-        def clip(step, first, last):
-            base = first // PAIR * PAIR
-            nc.gpsimd.tensor_scalar(step[:, first - base : last - base], neg_y[:, first:last], CLIP, -CLIP, ALU.min, ALU.max)
-
-        def scatter(t, step):
-            own = slice(t % 2 * S, (t % 2 + 1) * S)
-            nc.vector.tensor_tensor(table[t][:].indirect(ent_sb[:]), shrunk[t][:], step[:, own], ALU.add)
-            nc.sync.dma_start(out=out_rows[:, t, :], in_=table[t][:])
-
-        shrink(1)
-        shrink(2)
-        step_low = keep.tile([P, PAIR], F32, name="step_low")
-        clip(step_low, 0, S // 2)
-        clip(step_low, S // 2, PAIR)
-        scatter(0, step_low)
-        shrink(3)
-        step_high = keep.tile([P, PAIR], F32, name="step_high", tag="shrunk0")
-        clip(step_high, PAIR, 2 * PAIR)
-        scatter(1, step_low)
-        scatter(2, step_high)
-        scatter(3, step_high)
+            cols = slice(t * S + js.start, t * S + js.stop)
+            nc.scalar.activation(y_sb[:, cols], acc[n][:], COPY)
+            nc.gpsimd.tensor_scalar(step[:, js], y_sb[:, cols], CLIP, -CLIP, ALU.min, ALU.max)
+            nc.gpsimd.tensor_tensor(new[t][:, js], shrunk[t][:, js], step[:, js], ALU.subtract)
+            if js.stop == S:
+                nc.vector.tensor_copy(table[t][:].indirect(ent_sb[:]), new[t][:])
+                nc.sync.dma_start(out=out_rows[:, t, :], in_=table[t][:, :U])

@@ -26,7 +26,6 @@ GROUP = 16
 DECAY = 0.875
 CLIP = 0.75
 M_VECTOR = 80
-SCALE_LOADS_FIRST = 5
 
 
 def tile_picked_clipsgd_none_p_kernel(tc, x_words, x_scales, w1, par, offs, ent, out):
@@ -55,27 +54,25 @@ def tile_picked_clipsgd_none_p_kernel(tc, x_words, x_scales, w1, par, offs, ent,
                 in_=x_words[g].rearrange("p n r -> p (n r)").bitcast(I32),
             )
 
-        def load_scales(loads):
-            for g, i in loads:
+        def load_scales():
+            for q in range(P // QUAD):
                 nc.sync.dma_start(
-                    out=xs_all[QUAD_ROWS * g + i : P : QUAD, :].bitcast(I32),
-                    in_=x_scales[g, i : QUAD_ROWS * (P // QUAD) : QUAD_ROWS, :].bitcast(I32),
+                    out=xs_all[QUAD * q : QUAD * q + PASSES * QUAD_ROWS, :].bitcast(I32),
+                    in_=x_scales[:, QUAD_ROWS * q : QUAD_ROWS * (q + 1), :].bitcast(I32),
                 )
 
         def load_table(t):
             nc.sync.dma_start(out=table[t][:, :U], in_=par_rows[:, t, :])
 
-        scale_loads = [(g, i) for i in range(QUAD_ROWS) for g in range(PASSES)]
         nc.gpsimd.memset(xs_all[:].bitcast(I32), 0)
 
         load_w(0)
-        load_scales(scale_loads[:SCALE_LOADS_FIRST])
+        load_scales()
         nc.sync.dma_start(offs_sb[:], offs)
         load_x(0)
-        load_scales(scale_loads[SCALE_LOADS_FIRST:])
-        load_w(1)
         nc.sync.dma_start(ent_sb[:], ent)
         load_table(0)
+        load_w(1)
         load_x(1)
         for t in range(1, TILES):
             load_table(t)

@@ -26,6 +26,7 @@ GROUP = 16
 DECAY = 0.875
 CLIP = 0.75
 M_VECTOR = 80
+SCALE_LOADS_FIRST = 5
 
 
 def tile_picked_clipsgd_none_p_kernel(tc, x_words, x_scales, w1, par, offs, ent, out):
@@ -42,7 +43,7 @@ def tile_picked_clipsgd_none_p_kernel(tc, x_words, x_scales, w1, par, offs, ent,
         w_raw = [keep.tile([P, PACK, N], F32, name=f"w_raw{g}") for g in range(PASSES)]
         x_all = [keep.tile([P, T], U32, name=f"x_all{g}") for g in range(PASSES)]
         xs_all = keep.tile([P, T], U8, name="xs_all")
-        table = [keep.tile([P, U + S if t in (0, TILES - 1) else U], F32, name=f"table{t}") for t in range(TILES)]
+        table = [keep.tile([P, U + S // 2 if t < 2 else U], F32, name=f"table{t}") for t in range(TILES)]
 
         def load_w(g):
             rows = w1[g * K_PASS : (g + 1) * K_PASS, :]
@@ -54,25 +55,27 @@ def tile_picked_clipsgd_none_p_kernel(tc, x_words, x_scales, w1, par, offs, ent,
                 in_=x_words[g].rearrange("p n r -> p (n r)").bitcast(I32),
             )
 
-        def load_scales():
-            for q in range(P // QUAD):
+        def load_scales(loads):
+            for g, i in loads:
                 nc.sync.dma_start(
-                    out=xs_all[QUAD * q : QUAD * q + PASSES * QUAD_ROWS, :].bitcast(I32),
-                    in_=x_scales[:, QUAD_ROWS * q : QUAD_ROWS * (q + 1), :].bitcast(I32),
+                    out=xs_all[QUAD_ROWS * g + i : P : QUAD, :].bitcast(I32),
+                    in_=x_scales[g, i : QUAD_ROWS * (P // QUAD) : QUAD_ROWS, :].bitcast(I32),
                 )
 
         def load_table(t):
             nc.sync.dma_start(out=table[t][:, :U], in_=par_rows[:, t, :])
 
+        scale_loads = [(g, i) for i in range(QUAD_ROWS) for g in range(PASSES)]
         nc.gpsimd.memset(xs_all[:].bitcast(I32), 0)
 
         load_w(0)
-        load_scales()
+        load_scales(scale_loads[:SCALE_LOADS_FIRST])
         nc.sync.dma_start(offs_sb[:], offs)
         load_x(0)
+        load_scales(scale_loads[SCALE_LOADS_FIRST:])
+        load_w(1)
         nc.sync.dma_start(ent_sb[:], ent)
         load_table(0)
-        load_w(1)
         load_x(1)
         for t in range(1, TILES):
             load_table(t)
@@ -117,7 +120,7 @@ def tile_picked_clipsgd_none_p_kernel(tc, x_words, x_scales, w1, par, offs, ent,
         for n in range(len(pieces)):
             product(0, n)
 
-        shrunk = [keep.tile([P, S], F32, name=f"shrunk{t}") for t in range(TILES - 1)] + [table[0][:, U:]]
+        shrunk = [keep.tile([P, S], F32, name=f"shrunk{t}") for t in range(TILES - 1)]
 
         def shrink(t):
             nc.vector.tensor_scalar(shrunk[t][:], table[t][:].indirect(ent_sb[:]), DECAY, 0.0, ALU.mult, ALU.add)
@@ -131,14 +134,23 @@ def tile_picked_clipsgd_none_p_kernel(tc, x_words, x_scales, w1, par, offs, ent,
 
         y_sb = keep.tile([P, TILES * S], F32, name="y_sb")
         step = keep.tile([P, S], F32, name="step")
-        new = [table[TILES - 1][:, U:] if t == 1 else keep.tile([P, S], F32, name=f"new{t}") for t in range(TILES)]
-        for t in range(1, TILES):
+        new = [keep.tile([P, S], F32, name=f"new{t}") for t in range(TILES)]
+        for t in range(1, TILES - 1):
             shrink(t)
+        for h, js in enumerate(halves):
+            list_columns = slice(js.start // GROUP, js.stop // GROUP)
+            nc.vector.tensor_scalar(
+                table[h][:, U:], table[TILES - 1][:].indirect(ent_sb[:, list_columns]), DECAY, 0.0, ALU.mult, ALU.add
+            )
         for n, (t, js) in enumerate(pieces):
             cols = slice(t * S + js.start, t * S + js.stop)
             nc.scalar.activation(y_sb[:, cols], acc[n][:], COPY)
             nc.gpsimd.tensor_scalar(step[:, js], y_sb[:, cols], CLIP, -CLIP, ALU.min, ALU.max)
-            nc.gpsimd.tensor_tensor(new[t][:, js], shrunk[t][:, js], step[:, js], ALU.subtract)
+            if t < TILES - 1:
+                nc.gpsimd.tensor_tensor(new[t][:, js], shrunk[t][:, js], step[:, js], ALU.subtract)
+            else:
+                for h, half in enumerate(halves):
+                    nc.gpsimd.tensor_tensor(new[t][:, half], table[h][:, U:], step[:, half], ALU.subtract)
             if js.stop == S:
                 nc.vector.tensor_copy(table[t][:].indirect(ent_sb[:]), new[t][:])
                 nc.sync.dma_start(out=out_rows[:, t, :], in_=table[t][:, :U])

@@ -26,7 +26,6 @@ GROUP = 16
 DECAY = 0.875
 CLIP = 0.75
 M_VECTOR = 80
-SCALE_LOADS_FIRST = 5
 
 
 def tile_picked_clipsgd_none_p_kernel(tc, x_words, x_scales, w1, par, offs, ent, out):
@@ -40,10 +39,10 @@ def tile_picked_clipsgd_none_p_kernel(tc, x_words, x_scales, w1, par, offs, ent,
 
         offs_sb = keep.tile([P, S // GROUP], U16, name="offs_sb")
         ent_sb = keep.tile([P, S // GROUP], U16, name="ent_sb")
-        w_raw = [keep.tile([P, PACK, N], F32, name=f"w_raw{g}") for g in range(PASSES)]
-        x_all = [keep.tile([P, T], U32, name=f"x_all{g}") for g in range(PASSES)]
+        w_raw = [keep.tile([P, PACK, N], F32, name=f"w_raw{g}", tag=f"w_raw{g}") for g in range(PASSES)]
+        x_all = [keep.tile([P, T], U32, name="x_all0", tag="x_all0")]
         xs_all = keep.tile([P, T], U8, name="xs_all")
-        table = [keep.tile([P, U + S // 2 if t < 2 else U], F32, name=f"table{t}") for t in range(TILES)]
+        table = [keep.tile([P, U + S // 2], F32, name="table0")]
 
         def load_w(g):
             rows = w1[g * K_PASS : (g + 1) * K_PASS, :]
@@ -55,33 +54,28 @@ def tile_picked_clipsgd_none_p_kernel(tc, x_words, x_scales, w1, par, offs, ent,
                 in_=x_words[g].rearrange("p n r -> p (n r)").bitcast(I32),
             )
 
-        def load_scales(loads):
-            for g, i in loads:
+        def load_scales():
+            for g in range(PASSES):
                 nc.sync.dma_start(
-                    out=xs_all[QUAD_ROWS * g + i : P : QUAD, :].bitcast(I32),
-                    in_=x_scales[g, i : QUAD_ROWS * (P // QUAD) : QUAD_ROWS, :].bitcast(I32),
+                    out=xs_all[QUAD_ROWS * g : P : QUAD // QUAD_ROWS, :].bitcast(I32),
+                    in_=x_scales[g].bitcast(I32),
                 )
 
         def load_table(t):
             nc.sync.dma_start(out=table[t][:, :U], in_=par_rows[:, t, :])
 
-        scale_loads = [(g, i) for i in range(QUAD_ROWS) for g in range(PASSES)]
         nc.gpsimd.memset(xs_all[:].bitcast(I32), 0)
 
         load_w(0)
-        load_scales(scale_loads[:SCALE_LOADS_FIRST])
+        load_scales()
         nc.sync.dma_start(offs_sb[:], offs)
         load_x(0)
-        load_scales(scale_loads[SCALE_LOADS_FIRST:])
-        load_w(1)
         nc.sync.dma_start(ent_sb[:], ent)
         load_table(0)
-        load_x(1)
-        for t in range(1, TILES):
-            load_table(t)
+        load_w(1)
 
         x_scale = keep.tile([P, S], U8, name="x_scale", align_bytes=64)
-        w_bf = [keep.tile([P, TILES, P, PACK], BF16, name=f"w_bf{g}", align_bytes=64) for g in range(PASSES)]
+        w_bf = [keep.tile([P, TILES, P, PACK], BF16, name=f"w_bf{g}", tag=f"w_bf{g}", align_bytes=64) for g in range(PASSES)]
         w_codes = [keep.tile([P, N], U32, name=f"w_codes{g}", align_bytes=64) for g in range(PASSES)]
         w_scales = [keep.tile([P, N], U8, name=f"w_scales{g}", align_bytes=64) for g in range(PASSES)]
         x_codes = [keep.tile([P, S], U32, name=f"x_codes{g}", align_bytes=64) for g in range(PASSES)]
@@ -97,8 +91,22 @@ def tile_picked_clipsgd_none_p_kernel(tc, x_words, x_scales, w1, par, offs, ent,
                 in_=w_bf[g][:].rearrange("p t m j -> p (t m j)"),
             )
             if g == 0:
+                picked = keep.tile([P, S], U8, name="picked", tag="picked")
+                nc.vector.tensor_copy(picked[:], xs_all[:].indirect(offs_sb[:]))
+                nc.vector.tensor_copy(x_scale[:], picked[:])
+                for i in range(1, QUAD_ROWS):
+                    for a in range(PASSES):
+                        nc.sync.dma_start(
+                            out=x_scale[QUAD_ROWS * a + i : P : QUAD, :].bitcast(I32),
+                            in_=picked[QUAD_ROWS * a + QUAD // QUAD_ROWS * i : P : QUAD, :].bitcast(I32),
+                        )
                 nc.vector.tensor_copy(x_codes[0][:], x_all[0][:].indirect(offs_sb[:]))
-                nc.vector.tensor_copy(x_scale[:], xs_all[:].indirect(offs_sb[:]))
+
+        x_all.append(keep.tile([P, T], U32, name="x_all1", tag="w_bf0", align_bytes=64))
+        load_x(1)
+        for t, tag in ((1, "x_all0"), (2, "picked"), (3, "w_raw1")):
+            table.append(keep.tile([P, U + S // 2 if t < 2 else U], F32, name=f"table{t}", tag=tag))
+            load_table(t)
 
         halves = [slice(0, S // 2), slice(S // 2, S)]
         pieces = [(0, js) for js in halves] + [(t, slice(0, S)) for t in range(1, TILES)]

@@ -26,6 +26,7 @@ GROUP = 16
 DECAY = 0.875
 CLIP = 0.75
 M_VECTOR = 80
+BURST = 256
 
 
 def tile_picked_clipsgd_none_p_kernel(tc, x_words, x_scales, w1, par, offs, ent, out):
@@ -37,12 +38,12 @@ def tile_picked_clipsgd_none_p_kernel(tc, x_words, x_scales, w1, par, offs, ent,
         keep = ctx.enter_context(tc.tile_pool(name="keep", bufs=1))
         psum = ctx.enter_context(tc.psum_pool(name="psum", bufs=1))
 
-        offs_sb = keep.tile([P, S // GROUP], U16, name="offs_sb")
-        ent_sb = keep.tile([P, S // GROUP], U16, name="ent_sb")
-        w_raw = [keep.tile([P, PACK, N], F32, name=f"w_raw{g}", tag=f"w_raw{g}") for g in range(PASSES)]
-        x_all = [keep.tile([P, T], U32, name="x_all0", tag="x_all0")]
-        xs_all = keep.tile([P, T], U8, name="xs_all")
-        table = [keep.tile([P, U + S // 2], F32, name="table0")]
+        offs_sb = keep.tile([P, S // GROUP], U16, name="offs_sb", align_bytes=BURST)
+        ent_sb = keep.tile([P, S // GROUP], U16, name="ent_sb", align_bytes=BURST)
+        w_raw = [keep.tile([P, PACK, N], F32, name=f"w_raw{g}", tag=f"w_raw{g}", align_bytes=BURST) for g in range(PASSES)]
+        x_all = [keep.tile([P, T], U32, name="x_all0", tag="x_all0", align_bytes=BURST)]
+        xs_all = keep.tile([P, T], U8, name="xs_all", align_bytes=BURST)
+        table = [keep.tile([P, U + S // 2], F32, name="table0", align_bytes=BURST)]
 
         def load_w(g):
             rows = w1[g * K_PASS : (g + 1) * K_PASS, :]
@@ -74,11 +75,11 @@ def tile_picked_clipsgd_none_p_kernel(tc, x_words, x_scales, w1, par, offs, ent,
         load_table(0)
         load_w(1)
 
-        x_scale = keep.tile([P, S], U8, name="x_scale", align_bytes=64)
-        w_bf = [keep.tile([P, TILES, P, PACK], BF16, name=f"w_bf{g}", tag=f"w_bf{g}", align_bytes=64) for g in range(PASSES)]
-        w_codes = [keep.tile([P, N], U32, name=f"w_codes{g}", align_bytes=64) for g in range(PASSES)]
-        w_scales = [keep.tile([P, N], U8, name=f"w_scales{g}", align_bytes=64) for g in range(PASSES)]
-        x_codes = [keep.tile([P, S], U32, name=f"x_codes{g}", align_bytes=64) for g in range(PASSES)]
+        x_scale = keep.tile([P, S], U8, name="x_scale", align_bytes=BURST)
+        w_bf = [keep.tile([P, TILES, P, PACK], BF16, name=f"w_bf{g}", tag=f"w_bf{g}", align_bytes=BURST) for g in range(PASSES)]
+        w_codes = [keep.tile([P, N], U32, name=f"w_codes{g}", align_bytes=BURST) for g in range(PASSES)]
+        w_scales = [keep.tile([P, N], U8, name=f"w_scales{g}", align_bytes=BURST) for g in range(PASSES)]
+        x_codes = [keep.tile([P, S], U32, name=f"x_codes{g}", align_bytes=BURST) for g in range(PASSES)]
 
         for g in range(PASSES):
             dst = w_bf[g][:].rearrange("p t m j -> p m j t")
@@ -91,7 +92,7 @@ def tile_picked_clipsgd_none_p_kernel(tc, x_words, x_scales, w1, par, offs, ent,
                 in_=w_bf[g][:].rearrange("p t m j -> p (t m j)"),
             )
             if g == 0:
-                picked = keep.tile([P, S], U8, name="picked", tag="picked")
+                picked = keep.tile([P, S], U8, name="picked", tag="picked", align_bytes=BURST)
                 nc.vector.tensor_copy(picked[:], xs_all[:].indirect(offs_sb[:]))
                 nc.vector.tensor_copy(x_scale[:], picked[:])
                 for i in range(1, QUAD_ROWS):
@@ -102,10 +103,10 @@ def tile_picked_clipsgd_none_p_kernel(tc, x_words, x_scales, w1, par, offs, ent,
                         )
                 nc.vector.tensor_copy(x_codes[0][:], x_all[0][:].indirect(offs_sb[:]))
 
-        x_all.append(keep.tile([P, T], U32, name="x_all1", tag="w_bf0", align_bytes=64))
+        x_all.append(keep.tile([P, T], U32, name="x_all1", tag="w_bf0", align_bytes=BURST))
         load_x(1)
         for t, tag in ((1, "x_all0"), (2, "picked"), (3, "w_raw1")):
-            table.append(keep.tile([P, U + S // 2 if t < 2 else U], F32, name=f"table{t}", tag=tag))
+            table.append(keep.tile([P, U + S // 2 if t < 2 else U], F32, name=f"table{t}", tag=tag, align_bytes=BURST))
             load_table(t)
 
         halves = [slice(0, S // 2), slice(S // 2, S)]

@@ -20,13 +20,16 @@ PACK = 4
 K_PASS = P * PACK
 PASSES = K // K_PASS
 TILES = N // P
+LAST = TILES - 1
 QUAD = 32
 QUAD_ROWS = 4
+SPREAD = QUAD // QUAD_ROWS
 GROUP = 16
+SPARE = S // 2
 DECAY = 0.875
 CLIP = 0.75
-M_VECTOR = 80
-BURST = 256
+VECTOR_SETS = 80
+ALIGN = 256
 
 
 def tile_picked_clipsgd_none_p_kernel(tc, x_words, x_scales, w1, par, offs, ent, out):
@@ -38,12 +41,12 @@ def tile_picked_clipsgd_none_p_kernel(tc, x_words, x_scales, w1, par, offs, ent,
         keep = ctx.enter_context(tc.tile_pool(name="keep", bufs=1))
         psum = ctx.enter_context(tc.psum_pool(name="psum", bufs=1))
 
-        offs_sb = keep.tile([P, S // GROUP], U16, name="offs_sb", align_bytes=BURST)
-        ent_sb = keep.tile([P, S // GROUP], U16, name="ent_sb", align_bytes=BURST)
-        w_raw = [keep.tile([P, PACK, N], F32, name=f"w_raw{g}", tag=f"w_raw{g}", align_bytes=BURST) for g in range(PASSES)]
-        x_all = [keep.tile([P, T], U32, name="x_all0", tag="x_all0", align_bytes=BURST)]
-        xs_all = keep.tile([P, T], U8, name="xs_all", align_bytes=BURST)
-        table = [keep.tile([P, U + S // 2], F32, name="table0", align_bytes=BURST)]
+        offs_sb = keep.tile([P, S // GROUP], U16, name="offs_sb", align_bytes=ALIGN)
+        ent_sb = keep.tile([P, S // GROUP], U16, name="ent_sb", align_bytes=ALIGN)
+        w_raw = [keep.tile([P, PACK, N], F32, name=f"w_raw{g}", tag=f"w_raw{g}", align_bytes=ALIGN) for g in range(PASSES)]
+        x_all = [keep.tile([P, T], U32, name="x_all0", tag="x_all0", align_bytes=ALIGN)]
+        xs_all = keep.tile([P, T], U8, name="xs_all", align_bytes=ALIGN)
+        table = [keep.tile([P, U + SPARE], F32, name="table0", align_bytes=ALIGN)]
 
         def load_w(g):
             rows = w1[g * K_PASS : (g + 1) * K_PASS, :]
@@ -55,73 +58,74 @@ def tile_picked_clipsgd_none_p_kernel(tc, x_words, x_scales, w1, par, offs, ent,
                 in_=x_words[g].rearrange("p n r -> p (n r)").bitcast(I32),
             )
 
-        def load_scales():
-            for g in range(PASSES):
-                nc.sync.dma_start(
-                    out=xs_all[QUAD_ROWS * g : P : QUAD // QUAD_ROWS, :].bitcast(I32),
-                    in_=x_scales[g].bitcast(I32),
-                )
-
         def load_table(t):
             nc.sync.dma_start(out=table[t][:, :U], in_=par_rows[:, t, :])
+
+        def list_columns(entries):
+            return slice(entries.start // GROUP, entries.stop // GROUP)
 
         nc.gpsimd.memset(xs_all[:].bitcast(I32), 0)
 
         load_w(0)
-        load_scales()
+        for g in range(PASSES):
+            nc.sync.dma_start(out=xs_all[QUAD_ROWS * g : P : SPREAD, :].bitcast(I32), in_=x_scales[g].bitcast(I32))
         nc.sync.dma_start(offs_sb[:], offs)
         load_x(0)
         nc.sync.dma_start(ent_sb[:], ent)
         load_table(0)
         load_w(1)
 
-        x_scale = keep.tile([P, S], U8, name="x_scale", align_bytes=BURST)
-        w_bf = [keep.tile([P, TILES, P, PACK], BF16, name=f"w_bf{g}", tag=f"w_bf{g}", align_bytes=BURST) for g in range(PASSES)]
-        w_codes = [keep.tile([P, N], U32, name=f"w_codes{g}", align_bytes=BURST) for g in range(PASSES)]
-        w_scales = [keep.tile([P, N], U8, name=f"w_scales{g}", align_bytes=BURST) for g in range(PASSES)]
-        x_codes = [keep.tile([P, S], U32, name=f"x_codes{g}", align_bytes=BURST) for g in range(PASSES)]
+        x_scale = keep.tile([P, S], U8, name="x_scale", align_bytes=ALIGN)
+        w_bf = [keep.tile([P, TILES, P, PACK], BF16, name=f"w_bf{g}", tag=f"w_bf{g}", align_bytes=ALIGN) for g in range(PASSES)]
+        w_codes = [keep.tile([P, N], U32, name=f"w_codes{g}", align_bytes=ALIGN) for g in range(PASSES)]
+        w_scales = [keep.tile([P, N], U8, name=f"w_scales{g}", align_bytes=ALIGN) for g in range(PASSES)]
+        x_codes = [keep.tile([P, S], U32, name=f"x_codes{g}", align_bytes=ALIGN) for g in range(PASSES)]
 
-        for g in range(PASSES):
+        def quantise_w(g):
             dst = w_bf[g][:].rearrange("p t m j -> p m j t")
             src = w_raw[g][:].rearrange("p j (m t) -> p m j t", t=TILES)
-            nc.vector.tensor_copy(dst[:, :M_VECTOR], src[:, :M_VECTOR])
-            nc.scalar.activation(dst[:, M_VECTOR:], src[:, M_VECTOR:], COPY)
+            nc.vector.tensor_copy(dst[:, :VECTOR_SETS], src[:, :VECTOR_SETS])
+            nc.scalar.activation(dst[:, VECTOR_SETS:], src[:, VECTOR_SETS:], COPY)
             nc.vector.quantize_mx(
                 out=w_codes[g][:].bitcast(FP8X4),
                 scales=w_scales[g][:],
                 in_=w_bf[g][:].rearrange("p t m j -> p (t m j)"),
             )
-            if g == 0:
-                picked = keep.tile([P, S], U8, name="picked", tag="picked", align_bytes=BURST)
-                nc.vector.tensor_copy(picked[:], xs_all[:].indirect(offs_sb[:]))
-                nc.vector.tensor_copy(x_scale[:], picked[:])
-                for i in range(1, QUAD_ROWS):
-                    for a in range(PASSES):
-                        nc.sync.dma_start(
-                            out=x_scale[QUAD_ROWS * a + i : P : QUAD, :].bitcast(I32),
-                            in_=picked[QUAD_ROWS * a + QUAD // QUAD_ROWS * i : P : QUAD, :].bitcast(I32),
-                        )
-                nc.vector.tensor_copy(x_codes[0][:], x_all[0][:].indirect(offs_sb[:]))
 
-        x_all.append(keep.tile([P, T], U32, name="x_all1", tag="w_bf0", align_bytes=BURST))
+        quantise_w(0)
+
+        picked = keep.tile([P, S], U8, name="picked", tag="picked", align_bytes=ALIGN)
+        nc.vector.tensor_copy(picked[:], xs_all[:].indirect(offs_sb[:]))
+        nc.vector.tensor_copy(x_scale[:], picked[:])
+        for i in range(1, QUAD_ROWS):
+            for g in range(PASSES):
+                nc.sync.dma_start(
+                    out=x_scale[QUAD_ROWS * g + i : P : QUAD, :].bitcast(I32),
+                    in_=picked[QUAD_ROWS * g + SPREAD * i : P : QUAD, :].bitcast(I32),
+                )
+        nc.vector.tensor_copy(x_codes[0][:], x_all[0][:].indirect(offs_sb[:]))
+
+        quantise_w(1)
+
+        x_all.append(keep.tile([P, T], U32, name="x_all1", tag="w_bf0", align_bytes=ALIGN))
         load_x(1)
-        for t, tag in ((1, "x_all0"), (2, "picked"), (3, "w_raw1")):
-            table.append(keep.tile([P, U + S // 2 if t < 2 else U], F32, name=f"table{t}", tag=tag, align_bytes=BURST))
+        for t, columns, tag in ((1, U + SPARE, "x_all0"), (2, U, "picked"), (3, U, "w_raw1")):
+            table.append(keep.tile([P, columns], F32, name=f"table{t}", tag=tag, align_bytes=ALIGN))
             load_table(t)
 
         halves = [slice(0, S // 2), slice(S // 2, S)]
-        pieces = [(0, js) for js in halves] + [(t, slice(0, S)) for t in range(1, TILES)]
-        acc = [psum.tile([P, js.stop - js.start], F32, name=f"acc{n}") for n, (t, js) in enumerate(pieces)]
+        pieces = [(t, entries) for entries in halves for t in range(2)] + [(t, slice(0, S)) for t in range(2, TILES)]
+        acc = [psum.tile([P, entries.stop - entries.start], F32, name=f"acc{n}") for n, (t, entries) in enumerate(pieces)]
 
         def product(g, n):
-            t, js = pieces[n]
+            t, entries = pieces[n]
             features = slice(t * P, (t + 1) * P)
             nc.tensor.matmul_mx(
                 out=acc[n][:],
                 lhsT=w_codes[g][:, features].bitcast(FP8X4),
                 lhsT_scale=w_scales[g][:, features],
-                rhs=x_codes[g][:, js].bitcast(FP8X4),
-                rhs_scale=x_scale[QUAD_ROWS * g : P, js],
+                rhs=x_codes[g][:, entries].bitcast(FP8X4),
+                rhs_scale=x_scale[QUAD_ROWS * g : P, entries],
                 start=(g == 0),
                 stop=(g == PASSES - 1),
             )
@@ -129,37 +133,33 @@ def tile_picked_clipsgd_none_p_kernel(tc, x_words, x_scales, w1, par, offs, ent,
         for n in range(len(pieces)):
             product(0, n)
 
-        shrunk = [keep.tile([P, S], F32, name=f"shrunk{t}") for t in range(TILES - 1)]
+        shrunk = [keep.tile([P, S], F32, name=f"shrunk{t}") for t in range(LAST)]
 
-        def shrink(t):
-            nc.vector.tensor_scalar(shrunk[t][:], table[t][:].indirect(ent_sb[:]), DECAY, 0.0, ALU.mult, ALU.add)
+        def shrink(dst, t, offsets):
+            nc.vector.tensor_scalar(dst, table[t][:].indirect(offsets), DECAY, 0.0, ALU.mult, ALU.add)
 
-        shrink(0)
-        for js in halves:
-            list_columns = slice(js.start // GROUP, js.stop // GROUP)
-            nc.vector.tensor_copy(x_codes[1][:, js], x_all[1][:].indirect(offs_sb[:, list_columns]))
+        shrink(shrunk[0][:], 0, ent_sb[:])
+        nc.vector.tensor_copy(x_codes[1][:], x_all[1][:].indirect(offs_sb[:]))
         for n in range(len(pieces)):
             product(1, n)
 
         y_sb = keep.tile([P, TILES * S], F32, name="y_sb")
-        step = keep.tile([P, S], F32, name="step")
+        step_tile = keep.tile([P, S], F32, name="step")
         new = [keep.tile([P, S], F32, name=f"new{t}") for t in range(TILES)]
-        for t in range(1, TILES - 1):
-            shrink(t)
-        for h, js in enumerate(halves):
-            list_columns = slice(js.start // GROUP, js.stop // GROUP)
-            nc.vector.tensor_scalar(
-                table[h][:, U:], table[TILES - 1][:].indirect(ent_sb[:, list_columns]), DECAY, 0.0, ALU.mult, ALU.add
-            )
-        for n, (t, js) in enumerate(pieces):
-            cols = slice(t * S + js.start, t * S + js.stop)
-            nc.scalar.activation(y_sb[:, cols], acc[n][:], COPY)
-            nc.gpsimd.tensor_scalar(step[:, js], y_sb[:, cols], CLIP, -CLIP, ALU.min, ALU.max)
-            if t < TILES - 1:
-                nc.gpsimd.tensor_tensor(new[t][:, js], shrunk[t][:, js], step[:, js], ALU.subtract)
+        for t in range(1, LAST):
+            shrink(shrunk[t][:], t, ent_sb[:])
+        for h, entries in enumerate(halves):
+            shrink(table[h][:, U:], LAST, ent_sb[:, list_columns(entries)])
+        for n, (t, entries) in enumerate(pieces):
+            y_piece = y_sb[:, t * S + entries.start : t * S + entries.stop]
+            nc.scalar.activation(y_piece, acc[n][:], COPY)
+            step = step_tile[:, : entries.stop - entries.start]
+            nc.gpsimd.tensor_scalar(step, y_piece, CLIP, -CLIP, ALU.min, ALU.max)
+            if t < LAST:
+                nc.gpsimd.tensor_tensor(new[t][:, entries], shrunk[t][:, entries], step, ALU.subtract)
             else:
                 for h, half in enumerate(halves):
                     nc.gpsimd.tensor_tensor(new[t][:, half], table[h][:, U:], step[:, half], ALU.subtract)
-            if js.stop == S:
-                nc.vector.tensor_copy(table[t][:].indirect(ent_sb[:]), new[t][:])
+            nc.vector.tensor_copy(table[t][:].indirect(ent_sb[:, list_columns(entries)]), new[t][:, entries])
+            if entries.stop == S:
                 nc.sync.dma_start(out=out_rows[:, t, :], in_=table[t][:, :U])

@@ -46,7 +46,7 @@ def tile_picked_clipsgd_none_p_kernel(tc, x_words, x_scales, w1, par, offs, ent,
         w_raw = [keep.tile([P, PACK, N], F32, name=f"w_raw{g}", tag=f"w_raw{g}", align_bytes=ALIGN) for g in range(PASSES)]
         x_all = [keep.tile([P, T], U32, name="x_all0", tag="x_all0", align_bytes=ALIGN)]
         xs_all = keep.tile([P, T], U8, name="xs_all", align_bytes=ALIGN)
-        table = [keep.tile([P, U + SPARE], F32, name="table0", align_bytes=ALIGN)]
+        table = [keep.tile([P, U + 2 * SPARE], F32, name="table0", align_bytes=ALIGN)]
 
         def load_w(g):
             rows = w1[g * K_PASS : (g + 1) * K_PASS, :]
@@ -109,12 +109,16 @@ def tile_picked_clipsgd_none_p_kernel(tc, x_words, x_scales, w1, par, offs, ent,
 
         x_all.append(keep.tile([P, T], U32, name="x_all1", tag="w_bf0", align_bytes=ALIGN))
         load_x(1)
-        for t, columns, tag in ((1, U + SPARE, "x_all0"), (2, U, "picked"), (3, U, "w_raw1")):
+        for t, columns, tag in ((1, U + SPARE, "x_all0"), (2, U, "w_raw1"), (3, U, "picked")):
             table.append(keep.tile([P, columns], F32, name=f"table{t}", tag=tag, align_bytes=ALIGN))
+        for t in (1, 3, 2):
             load_table(t)
 
         halves = [slice(0, S // 2), slice(S // 2, S)]
-        pieces = [(t, entries) for entries in halves for t in range(2)] + [(t, slice(0, S)) for t in range(2, TILES)]
+        quarters = [slice(0, S // 4), slice(S // 4, S // 2)]
+        whole = [(t, slice(0, S)) for t in (3, 2)]
+        pieces = [(0, quarters[0]), (1, halves[0]), (0, quarters[1]), (0, halves[1]), (1, halves[1])] + whole
+        steps = [(0, quarters[0]), (1, halves[0]), (0, slice(S // 4, S)), (1, halves[1])] + whole
         acc = [psum.tile([P, entries.stop - entries.start], F32, name=f"acc{n}") for n, (t, entries) in enumerate(pieces)]
 
         def product(g, n):
@@ -139,27 +143,36 @@ def tile_picked_clipsgd_none_p_kernel(tc, x_words, x_scales, w1, par, offs, ent,
             nc.vector.tensor_scalar(dst, table[t][:].indirect(offsets), DECAY, 0.0, ALU.mult, ALU.add)
 
         shrink(shrunk[0][:], 0, ent_sb[:])
-        nc.vector.tensor_copy(x_codes[1][:], x_all[1][:].indirect(offs_sb[:]))
+        for entries in halves:
+            nc.vector.tensor_copy(x_codes[1][:, entries], x_all[1][:].indirect(offs_sb[:, list_columns(entries)]))
         for n in range(len(pieces)):
             product(1, n)
 
         y_sb = keep.tile([P, TILES * S], F32, name="y_sb")
         step_tile = keep.tile([P, S], F32, name="step")
         new = [keep.tile([P, S], F32, name=f"new{t}") for t in range(TILES)]
-        for t in range(1, LAST):
-            shrink(shrunk[t][:], t, ent_sb[:])
-        for h, entries in enumerate(halves):
-            shrink(table[h][:, U:], LAST, ent_sb[:, list_columns(entries)])
+        shrink(shrunk[1][:], 1, ent_sb[:])
+        late = {3: [table[0][:, U : U + SPARE], shrunk[2][:, halves[0]]], 2: [table[1][:, U:], table[0][:, U + SPARE :]]}
+
+        def shrink_late(t):
+            for h, entries in enumerate(halves):
+                shrink(late[t][h], t, ent_sb[:, list_columns(entries)])
+
+        shrink_late(3)
         for n, (t, entries) in enumerate(pieces):
             y_piece = y_sb[:, t * S + entries.start : t * S + entries.stop]
             nc.scalar.activation(y_piece, acc[n][:], COPY)
+        for n, (t, entries) in enumerate(steps):
+            y_piece = y_sb[:, t * S + entries.start : t * S + entries.stop]
             step = step_tile[:, : entries.stop - entries.start]
             nc.gpsimd.tensor_scalar(step, y_piece, CLIP, -CLIP, ALU.min, ALU.max)
-            if t < LAST:
+            if t < 2:
                 nc.gpsimd.tensor_tensor(new[t][:, entries], shrunk[t][:, entries], step, ALU.subtract)
             else:
-                for h, half in enumerate(halves):
-                    nc.gpsimd.tensor_tensor(new[t][:, half], table[h][:, U:], step[:, half], ALU.subtract)
+                for h in (1, 0):
+                    nc.gpsimd.tensor_tensor(new[t][:, halves[h]], late[t][h], step[:, halves[h]], ALU.subtract)
             nc.vector.tensor_copy(table[t][:].indirect(ent_sb[:, list_columns(entries)]), new[t][:, entries])
+            if n == 0:
+                shrink_late(2)
             if entries.stop == S:
                 nc.sync.dma_start(out=out_rows[:, t, :], in_=table[t][:, :U])

@@ -20,12 +20,10 @@ PACK = 4
 K_PASS = P * PACK
 PASSES = K // K_PASS
 TILES = N // P
-LAST = TILES - 1
 QUAD = 32
 QUAD_ROWS = 4
 SPREAD = QUAD // QUAD_ROWS
 GROUP = 16
-SPARE = S // 2
 DECAY = 0.875
 CLIP = 0.75
 VECTOR_SETS = 80
@@ -46,33 +44,29 @@ def tile_picked_clipsgd_none_p_kernel(tc, x_words, x_scales, w1, par, offs, ent,
         w_raw = [keep.tile([P, PACK, N], F32, name=f"w_raw{g}", tag=f"w_raw{g}", align_bytes=ALIGN) for g in range(PASSES)]
         x_all = [keep.tile([P, T], U32, name="x_all0", tag="x_all0", align_bytes=ALIGN)]
         xs_all = keep.tile([P, T], U8, name="xs_all", align_bytes=ALIGN)
-        table = [keep.tile([P, U + 2 * SPARE], F32, name="table0", align_bytes=ALIGN)]
 
         def load_w(g):
             rows = w1[g * K_PASS : (g + 1) * K_PASS, :]
             nc.sync.dma_start(out=w_raw[g][:], in_=rows.rearrange("(p j) c -> p j c", j=PACK))
 
-        def load_x(g):
+        def load_x(g, columns):
             nc.sync.dma_start(
-                out=x_all[g][:].bitcast(I32),
-                in_=x_words[g].rearrange("p n r -> p (n r)").bitcast(I32),
+                out=x_all[g][:].bitcast(I32)[:, columns],
+                in_=x_words[g].rearrange("p n r -> p (n r)").bitcast(I32)[:, columns],
             )
-
-        def load_table(t):
-            nc.sync.dma_start(out=table[t][:, :U], in_=par_rows[:, t, :])
 
         def list_columns(entries):
             return slice(entries.start // GROUP, entries.stop // GROUP)
 
         nc.gpsimd.memset(xs_all[:].bitcast(I32), 0)
 
-        load_w(0)
+        load_x(0, slice(0, T // 2))
         for g in range(PASSES):
             nc.sync.dma_start(out=xs_all[QUAD_ROWS * g : P : SPREAD, :].bitcast(I32), in_=x_scales[g].bitcast(I32))
         nc.sync.dma_start(offs_sb[:], offs)
-        load_x(0)
         nc.sync.dma_start(ent_sb[:], ent)
-        load_table(0)
+        load_w(0)
+        load_x(0, slice(T // 2, T))
         load_w(1)
 
         x_scale = keep.tile([P, S], U8, name="x_scale", align_bytes=ALIGN)
@@ -92,33 +86,27 @@ def tile_picked_clipsgd_none_p_kernel(tc, x_words, x_scales, w1, par, offs, ent,
                 in_=w_bf[g][:].rearrange("p t m j -> p (t m j)"),
             )
 
-        quantise_w(0)
-
         picked = keep.tile([P, S], U8, name="picked", tag="picked", align_bytes=ALIGN)
         nc.vector.tensor_copy(picked[:], xs_all[:].indirect(offs_sb[:]))
-        nc.vector.tensor_copy(x_scale[:], picked[:])
+        nc.vector.tensor_copy(x_scale[:].bitcast(I32), picked[:].bitcast(I32))
         for i in range(1, QUAD_ROWS):
             for g in range(PASSES):
                 nc.sync.dma_start(
                     out=x_scale[QUAD_ROWS * g + i : P : QUAD, :].bitcast(I32),
                     in_=picked[QUAD_ROWS * g + SPREAD * i : P : QUAD, :].bitcast(I32),
                 )
+        quantise_w(0)
         nc.vector.tensor_copy(x_codes[0][:], x_all[0][:].indirect(offs_sb[:]))
-
         quantise_w(1)
 
-        x_all.append(keep.tile([P, T], U32, name="x_all1", tag="w_bf0", align_bytes=ALIGN))
-        load_x(1)
-        for t, columns, tag in ((1, U + SPARE, "x_all0"), (2, U, "w_raw1"), (3, U, "picked")):
-            table.append(keep.tile([P, columns], F32, name=f"table{t}", tag=tag, align_bytes=ALIGN))
-        for t in (1, 3, 2):
-            load_table(t)
+        x_all.append(keep.tile([P, T], U32, name="x_all1", tag="w_raw0", align_bytes=ALIGN))
+        load_x(1, slice(0, T))
+        table = [keep.tile([P, U], F32, name=f"table{t}", tag=tag, align_bytes=ALIGN) for t, tag in enumerate(("w_bf0", "x_all0", "w_raw1"))]
+        for t in range(3):
+            nc.sync.dma_start(out=table[t][:], in_=par_rows[:, t, :])
 
         halves = [slice(0, S // 2), slice(S // 2, S)]
-        quarters = [slice(0, S // 4), slice(S // 4, S // 2)]
-        whole = [(t, slice(0, S)) for t in (3, 2)]
-        pieces = [(0, quarters[0]), (1, halves[0]), (0, quarters[1]), (0, halves[1]), (1, halves[1])] + whole
-        steps = [(0, quarters[0]), (1, halves[0]), (0, slice(S // 4, S)), (1, halves[1])] + whole
+        pieces = [(t + u, entries) for t in (0, 2) for entries in halves for u in range(2)]
         acc = [psum.tile([P, entries.stop - entries.start], F32, name=f"acc{n}") for n, (t, entries) in enumerate(pieces)]
 
         def product(g, n):
@@ -136,43 +124,58 @@ def tile_picked_clipsgd_none_p_kernel(tc, x_words, x_scales, w1, par, offs, ent,
 
         for n in range(len(pieces)):
             product(0, n)
-
-        shrunk = [keep.tile([P, S], F32, name=f"shrunk{t}") for t in range(LAST)]
-
-        def shrink(dst, t, offsets):
-            nc.vector.tensor_scalar(dst, table[t][:].indirect(offsets), DECAY, 0.0, ALU.mult, ALU.add)
-
-        shrink(shrunk[0][:], 0, ent_sb[:])
         for entries in halves:
             nc.vector.tensor_copy(x_codes[1][:, entries], x_all[1][:].indirect(offs_sb[:, list_columns(entries)]))
         for n in range(len(pieces)):
             product(1, n)
 
-        y_sb = keep.tile([P, TILES * S], F32, name="y_sb")
-        step_tile = keep.tile([P, S], F32, name="step")
+        table.append(keep.tile([P, U], F32, name="table3", tag="w_bf1", align_bytes=ALIGN))
+        nc.sync.dma_start(out=table[3][:], in_=par_rows[:, 3, :])
+
+        y_sb = keep.tile([P, S // 2], F32, name="y_sb")
+        step_sb = keep.tile([P, S // 2], F32, name="step_sb")
+        left = keep.tile([P, S], F32, name="left")
+        right = keep.tile([P, S], F32, name="right")
         new = [keep.tile([P, S], F32, name=f"new{t}") for t in range(TILES)]
-        shrink(shrunk[1][:], 1, ent_sb[:])
-        late = {3: [table[0][:, U : U + SPARE], shrunk[2][:, halves[0]]], 2: [table[1][:, U:], table[0][:, U + SPARE :]]}
+        shrunk = [left[:, halves[0]], right[:, halves[0]], right[:, halves[0]], left[:, halves[1]]]
+        shrunk += [right[:, halves[0]], left[:, halves[0]], right[:, halves[1]], left[:, halves[1]]]
+        step = [step_sb[:], y_sb[:]] + [step_sb[:]] * 6
 
-        def shrink_late(t):
-            for h, entries in enumerate(halves):
-                shrink(late[t][h], t, ent_sb[:, list_columns(entries)])
+        def look_up(dst, t, entries):
+            nc.scalar.activation(dst, table[t][:].indirect(ent_sb[:, list_columns(entries)]), COPY, scale=DECAY)
 
-        shrink_late(3)
-        for n, (t, entries) in enumerate(pieces):
-            y_piece = y_sb[:, t * S + entries.start : t * S + entries.stop]
-            nc.scalar.activation(y_piece, acc[n][:], COPY)
-        for n, (t, entries) in enumerate(steps):
-            y_piece = y_sb[:, t * S + entries.start : t * S + entries.stop]
-            step = step_tile[:, : entries.stop - entries.start]
-            nc.gpsimd.tensor_scalar(step, y_piece, CLIP, -CLIP, ALU.min, ALU.max)
-            if t < 2:
-                nc.gpsimd.tensor_tensor(new[t][:, entries], shrunk[t][:, entries], step, ALU.subtract)
+        def clip(n):
+            if n < 2:
+                nc.vector.tensor_scalar(step[n], acc[n][:], CLIP, -CLIP, ALU.min, ALU.max)
             else:
-                for h in (1, 0):
-                    nc.gpsimd.tensor_tensor(new[t][:, halves[h]], late[t][h], step[:, halves[h]], ALU.subtract)
-            nc.vector.tensor_copy(table[t][:].indirect(ent_sb[:, list_columns(entries)]), new[t][:, entries])
+                nc.scalar.activation(y_sb[:], acc[n][:], COPY)
+                nc.gpsimd.tensor_scalar(step[n], y_sb[:], CLIP, -CLIP, ALU.min, ALU.max)
+
+        def put(n):
+            t, entries = pieces[n]
+            engine = nc.vector if n == 0 else nc.gpsimd
+            engine.tensor_tensor(new[t][:, entries], shrunk[n], step[n], ALU.subtract)
             if n == 0:
-                shrink_late(2)
+                clip(1)
+            nc.vector.tensor_copy(table[t][:].indirect(ent_sb[:, list_columns(entries)]), new[t][:, entries])
             if entries.stop == S:
-                nc.sync.dma_start(out=out_rows[:, t, :], in_=table[t][:, :U])
+                nc.sync.dma_start(out=out_rows[:, t, :], in_=table[t][:])
+
+        look_up(shrunk[0], 0, halves[0])
+        clip(0)
+        put(0)
+        look_up(shrunk[1], 1, halves[0])
+        look_up(shrunk[3], 1, halves[1])
+        put(1)
+        clip(2)
+        look_up(shrunk[2], 0, halves[1])
+        put(2)
+        clip(3)
+        look_up(right[:], 2, slice(0, S))
+        put(3)
+        clip(4)
+        look_up(left[:], 3, slice(0, S))
+        put(4)
+        for n in range(5, len(pieces)):
+            clip(n)
+            put(n)

@@ -106,7 +106,8 @@ def tile_picked_clipsgd_none_p_kernel(tc, x_words, x_scales, w1, par, offs, ent,
             nc.sync.dma_start(out=table[t][:], in_=par_rows[:, t, :])
 
         halves = [slice(0, S // 2), slice(S // 2, S)]
-        pieces = [(t + u, entries) for t in (0, 2) for entries in halves for u in range(2)]
+        first, second = halves
+        pieces = [(0, first), (1, first), (2, first), (0, second), (1, second), (3, first), (2, second), (3, second)]
         acc = [psum.tile([P, entries.stop - entries.start], F32, name=f"acc{n}") for n, (t, entries) in enumerate(pieces)]
 
         def product(g, n):
@@ -132,50 +133,66 @@ def tile_picked_clipsgd_none_p_kernel(tc, x_words, x_scales, w1, par, offs, ent,
         table.append(keep.tile([P, U], F32, name="table3", tag="w_bf1", align_bytes=ALIGN))
         nc.sync.dma_start(out=table[3][:], in_=par_rows[:, 3, :])
 
-        y_sb = keep.tile([P, S // 2], F32, name="y_sb")
-        step_sb = keep.tile([P, S // 2], F32, name="step_sb")
-        left = keep.tile([P, S], F32, name="left")
-        right = keep.tile([P, S], F32, name="right")
+        H = S // 2
+        Q = H // 2
+        steps = [keep.tile([P, H], F32, name=f"step{n}") for n in range(2)]
+        second_piece = keep.tile([P, S], F32, name="second_piece")
+        y_sb = second_piece[:, :H]
+        looked = [keep.tile([P, H], F32, name=f"looked{n}") for n in range(4)]
         new = [keep.tile([P, S], F32, name=f"new{t}") for t in range(TILES)]
-        shrunk = [left[:, halves[0]], right[:, halves[0]], right[:, halves[0]], left[:, halves[1]]]
-        shrunk += [right[:, halves[0]], left[:, halves[0]], right[:, halves[1]], left[:, halves[1]]]
-        step = [step_sb[:], y_sb[:]] + [step_sb[:]] * 6
+        shrunk = [looked[n][:] for n in (0, 0, 1, 1, 2, 1, 3, 2)]
+        shrunk[1] = second_piece[:, Q : Q + H]
+        step = [steps[n % 2] for n in range(len(pieces))]
 
-        def look_up(dst, t, entries):
-            nc.scalar.activation(dst, table[t][:].indirect(ent_sb[:, list_columns(entries)]), COPY, scale=DECAY)
+        def look_up(n):
+            t, entries = pieces[n]
+            nc.scalar.activation(shrunk[n], table[t][:].indirect(ent_sb[:, list_columns(entries)]), COPY, scale=DECAY)
 
         def clip(n):
-            if n < 2:
-                nc.vector.tensor_scalar(step[n], acc[n][:], CLIP, -CLIP, ALU.min, ALU.max)
-            else:
-                nc.scalar.activation(y_sb[:], acc[n][:], COPY)
-                nc.gpsimd.tensor_scalar(step[n], y_sb[:], CLIP, -CLIP, ALU.min, ALU.max)
+            nc.scalar.activation(y_sb, acc[n][:], COPY)
+            nc.gpsimd.tensor_scalar(step[n][:], y_sb, CLIP, -CLIP, ALU.min, ALU.max)
 
-        def put(n):
+        def clip_from_bank(dst, src):
+            nc.vector.tensor_scalar(dst, src, CLIP, -CLIP, ALU.min, ALU.max)
+
+        def subtract(n, engine):
             t, entries = pieces[n]
-            engine = nc.vector if n == 0 else nc.gpsimd
-            engine.tensor_tensor(new[t][:, entries], shrunk[n], step[n], ALU.subtract)
-            if n == 0:
-                clip(1)
+            engine.tensor_tensor(new[t][:, entries], shrunk[n], step[n][:], ALU.subtract)
+
+        def scatter(n):
+            t, entries = pieces[n]
             nc.vector.tensor_copy(table[t][:].indirect(ent_sb[:, list_columns(entries)]), new[t][:, entries])
             if entries.stop == S:
                 nc.sync.dma_start(out=out_rows[:, t, :], in_=table[t][:])
 
-        look_up(shrunk[0], 0, halves[0])
-        clip(0)
-        put(0)
-        look_up(shrunk[1], 1, halves[0])
-        look_up(shrunk[3], 1, halves[1])
-        put(1)
+        look_up(0)
+        clip_from_bank(step[0][:], acc[0][:])
+        clip_from_bank(second_piece[:, :Q], acc[1][:, :Q])
+        subtract(0, nc.vector)
+        clip_from_bank(second_piece[:, Q + H :], acc[1][:, Q:])
+        scatter(0)
+        look_up(1)
+        look_up(4)
+        nc.gpsimd.tensor_tensor(new[1][:, :Q], second_piece[:, Q:H], second_piece[:, :Q], ALU.subtract)
+        nc.gpsimd.tensor_tensor(new[1][:, Q:H], second_piece[:, H : H + Q], second_piece[:, H + Q :], ALU.subtract)
+        scatter(1)
         clip(2)
-        look_up(shrunk[2], 0, halves[1])
-        put(2)
+        look_up(2)
         clip(3)
-        look_up(right[:], 2, slice(0, S))
-        put(3)
+        look_up(6)
+        subtract(2, nc.gpsimd)
+        scatter(2)
         clip(4)
-        look_up(left[:], 3, slice(0, S))
-        put(4)
+        look_up(3)
+        subtract(3, nc.gpsimd)
+        scatter(3)
+        clip(5)
+        look_up(5)
+        subtract(4, nc.gpsimd)
+        scatter(4)
+        look_up(7)
         for n in range(5, len(pieces)):
-            clip(n)
-            put(n)
+            if n + 1 < len(pieces):
+                clip(n + 1)
+            subtract(n, nc.gpsimd)
+            scatter(n)

@@ -134,30 +134,24 @@ def tile_picked_clipsgd_none_p_kernel(tc, x_words, x_scales, w1, par, offs, ent,
         nc.sync.dma_start(out=table[3][:], in_=par_rows[:, 3, :])
 
         H = S // 2
-        Q = H // 2
-        steps = [keep.tile([P, H], F32, name=f"step{n}") for n in range(2)]
-        second_piece = keep.tile([P, S], F32, name="second_piece")
-        y_sb = second_piece[:, :H]
-        looked = [keep.tile([P, H], F32, name=f"looked{n}") for n in range(4)]
+        steps = [keep.tile([P, H], F32, name=f"step{n}") for n in range(3)]
+        y_sb = steps[1]
+        looked = [keep.tile([P, H], F32, name=f"looked{n}") for n in range(5)]
         new = [keep.tile([P, S], F32, name=f"new{t}") for t in range(TILES)]
-        shrunk = [looked[n][:] for n in (0, 0, 1, 1, 2, 1, 3, 2)]
-        shrunk[1] = second_piece[:, Q : Q + H]
-        step = [steps[n % 2] for n in range(len(pieces))]
+        shrunk = [looked[n] for n in (0, 4, 1, 1, 2, 1, 3, 2)]
+        step = [steps[n] for n in (0, 1, 2, 0, 2, 0, 2, 0)]
 
         def look_up(n):
             t, entries = pieces[n]
-            nc.scalar.activation(shrunk[n], table[t][:].indirect(ent_sb[:, list_columns(entries)]), COPY, scale=DECAY)
+            nc.scalar.activation(shrunk[n][:], table[t][:].indirect(ent_sb[:, list_columns(entries)]), COPY, scale=DECAY)
 
         def clip(n):
-            nc.scalar.activation(y_sb, acc[n][:], COPY)
-            nc.gpsimd.tensor_scalar(step[n][:], y_sb, CLIP, -CLIP, ALU.min, ALU.max)
-
-        def clip_from_bank(dst, src):
-            nc.vector.tensor_scalar(dst, src, CLIP, -CLIP, ALU.min, ALU.max)
+            nc.scalar.activation(y_sb[:], acc[n][:], COPY)
+            nc.gpsimd.tensor_scalar(step[n][:], y_sb[:], CLIP, -CLIP, ALU.min, ALU.max)
 
         def subtract(n, engine):
             t, entries = pieces[n]
-            engine.tensor_tensor(new[t][:, entries], shrunk[n], step[n][:], ALU.subtract)
+            engine.tensor_tensor(new[t][:, entries], shrunk[n][:], step[n][:], ALU.subtract)
 
         def scatter(n):
             t, entries = pieces[n]
@@ -166,20 +160,17 @@ def tile_picked_clipsgd_none_p_kernel(tc, x_words, x_scales, w1, par, offs, ent,
                 nc.sync.dma_start(out=out_rows[:, t, :], in_=table[t][:])
 
         look_up(0)
-        clip_from_bank(step[0][:], acc[0][:])
-        clip_from_bank(second_piece[:, :Q], acc[1][:, :Q])
+        for n in range(3):
+            nc.vector.tensor_scalar(step[n][:], acc[n][:], CLIP, -CLIP, ALU.min, ALU.max)
         subtract(0, nc.vector)
-        clip_from_bank(second_piece[:, Q + H :], acc[1][:, Q:])
         scatter(0)
         look_up(1)
         look_up(4)
-        nc.gpsimd.tensor_tensor(new[1][:, :Q], second_piece[:, Q:H], second_piece[:, :Q], ALU.subtract)
-        nc.gpsimd.tensor_tensor(new[1][:, Q:H], second_piece[:, H : H + Q], second_piece[:, H + Q :], ALU.subtract)
+        subtract(1, nc.gpsimd)
         scatter(1)
-        clip(2)
         look_up(2)
-        clip(3)
         look_up(6)
+        clip(3)
         subtract(2, nc.gpsimd)
         scatter(2)
         clip(4)

@@ -135,11 +135,11 @@ def tile_picked_clipsgd_none_p_kernel(tc, x_words, x_scales, w1, par, offs, ent,
 
         H = S // 2
         steps = [keep.tile([P, H], F32, name=f"step{n}") for n in range(3)]
-        y_sb = steps[1]
+        y_sb = steps[2]
         looked = [keep.tile([P, H], F32, name=f"looked{n}") for n in range(5)]
         new = [keep.tile([P, S], F32, name=f"new{t}") for t in range(TILES)]
         shrunk = [looked[n] for n in (0, 4, 1, 1, 2, 1, 3, 2)]
-        step = [steps[n] for n in (0, 1, 2, 0, 2, 0, 2, 0)]
+        step = [steps[n] for n in (0, 1, 2, 0, 1, 0, 1, 0)]
 
         def look_up(n):
             t, entries = pieces[n]
@@ -170,11 +170,11 @@ def tile_picked_clipsgd_none_p_kernel(tc, x_words, x_scales, w1, par, offs, ent,
         scatter(1)
         look_up(2)
         look_up(6)
-        clip(3)
         subtract(2, nc.gpsimd)
         scatter(2)
-        clip(4)
+        clip(3)
         look_up(3)
+        clip(4)
         subtract(3, nc.gpsimd)
         scatter(3)
         clip(5)

@@ -69,7 +69,7 @@ def tile_picked_clipsgd_none_p_kernel(tc, x_words, x_scales, w1, par, offs, ent,
         load_x(0, slice(T // 2, T))
         load_w(1)
 
-        x_scale = keep.tile([P, S], U8, name="x_scale", align_bytes=ALIGN)
+        x_scale = [keep.tile([P, S], U8, name=f"x_scale{g}", align_bytes=ALIGN) for g in range(PASSES)]
         w_bf = [keep.tile([P, TILES, P, PACK], BF16, name=f"w_bf{g}", tag=f"w_bf{g}", align_bytes=ALIGN) for g in range(PASSES)]
         w_codes = [keep.tile([P, N], U32, name=f"w_codes{g}", align_bytes=ALIGN) for g in range(PASSES)]
         w_scales = [keep.tile([P, N], U8, name=f"w_scales{g}", align_bytes=ALIGN) for g in range(PASSES)]
@@ -88,19 +88,24 @@ def tile_picked_clipsgd_none_p_kernel(tc, x_words, x_scales, w1, par, offs, ent,
 
         picked = keep.tile([P, S], U8, name="picked", tag="picked", align_bytes=ALIGN)
         nc.vector.tensor_copy(picked[:], xs_all[:].indirect(offs_sb[:]))
-        nc.vector.tensor_copy(x_scale[:].bitcast(I32), picked[:].bitcast(I32))
-        for i in range(1, QUAD_ROWS):
-            for g in range(PASSES):
+        for g in range(PASSES):
+            nc.vector.tensor_copy(x_scale[g][:].bitcast(I32), picked[:].bitcast(I32))
+
+        def move_scale_rows(g):
+            for i in range(1, QUAD_ROWS):
                 nc.sync.dma_start(
-                    out=x_scale[QUAD_ROWS * g + i : P : QUAD, :].bitcast(I32),
-                    in_=picked[QUAD_ROWS * g + SPREAD * i : P : QUAD, :].bitcast(I32),
+                    out=x_scale[g][QUAD_ROWS * g + i : P : QUAD, :].bitcast(I32),
+                    in_=x_scale[1 - g][QUAD_ROWS * g + SPREAD * i : P : QUAD, :].bitcast(I32),
                 )
+
+        move_scale_rows(0)
+        x_all.append(keep.tile([P, T], U32, name="x_all1", tag="picked", align_bytes=ALIGN))
+        load_x(1, slice(0, T))
+        move_scale_rows(1)
         quantise_w(0)
         nc.vector.tensor_copy(x_codes[0][:], x_all[0][:].indirect(offs_sb[:]))
         quantise_w(1)
 
-        x_all.append(keep.tile([P, T], U32, name="x_all1", tag="w_raw0", align_bytes=ALIGN))
-        load_x(1, slice(0, T))
         table = [keep.tile([P, U], F32, name=f"table{t}", tag=tag, align_bytes=ALIGN) for t, tag in enumerate(("w_bf0", "x_all0", "w_raw1"))]
         for t in range(3):
             nc.sync.dma_start(out=table[t][:], in_=par_rows[:, t, :])
@@ -118,7 +123,7 @@ def tile_picked_clipsgd_none_p_kernel(tc, x_words, x_scales, w1, par, offs, ent,
                 lhsT=w_codes[g][:, features].bitcast(FP8X4),
                 lhsT_scale=w_scales[g][:, features],
                 rhs=x_codes[g][:, entries].bitcast(FP8X4),
-                rhs_scale=x_scale[QUAD_ROWS * g : P, entries],
+                rhs_scale=x_scale[g][QUAD_ROWS * g : P, entries],
                 start=(g == 0),
                 stop=(g == PASSES - 1),
             )

@@ -27,7 +27,9 @@ GROUP = 16
 DECAY = 0.875
 CLIP = 0.75
 VECTOR_SETS = 80
+VECTOR_CLIPS = 2
 ALIGN = 256
+H = S // 2
 
 
 def tile_picked_clipsgd_none_p_kernel(tc, x_words, x_scales, w1, par, offs, ent, out):
@@ -37,12 +39,13 @@ def tile_picked_clipsgd_none_p_kernel(tc, x_words, x_scales, w1, par, offs, ent,
 
     with ExitStack() as ctx:
         keep = ctx.enter_context(tc.tile_pool(name="keep", bufs=1))
+        laid = ctx.enter_context(tc.tile_pool(name="laid", bufs=1))
         psum = ctx.enter_context(tc.psum_pool(name="psum", bufs=1))
 
         offs_sb = keep.tile([P, S // GROUP], U16, name="offs_sb", align_bytes=ALIGN)
         ent_sb = keep.tile([P, S // GROUP], U16, name="ent_sb", align_bytes=ALIGN)
         w_raw = [keep.tile([P, PACK, N], F32, name=f"w_raw{g}", tag=f"w_raw{g}", align_bytes=ALIGN) for g in range(PASSES)]
-        x_all = [keep.tile([P, T], U32, name="x_all0", tag="x_all0", align_bytes=ALIGN)]
+        x_all = [laid.tile([P, T], U32, name="x_all0", align_bytes=ALIGN, offset=0)]
         xs_all = keep.tile([P, T], U8, name="xs_all", align_bytes=ALIGN)
 
         def load_w(g):
@@ -74,12 +77,16 @@ def tile_picked_clipsgd_none_p_kernel(tc, x_words, x_scales, w1, par, offs, ent,
         w_codes = [keep.tile([P, N], U32, name=f"w_codes{g}", align_bytes=ALIGN) for g in range(PASSES)]
         w_scales = [keep.tile([P, N], U8, name=f"w_scales{g}", align_bytes=ALIGN) for g in range(PASSES)]
         x_codes = [keep.tile([P, S], U32, name=f"x_codes{g}", align_bytes=ALIGN) for g in range(PASSES)]
+        halves = [slice(0, H), slice(H, S)]
+        first, second = halves
 
-        def quantise_w(g):
+        def cast_w(g):
             dst = w_bf[g][:].rearrange("p t m j -> p m j t")
             src = w_raw[g][:].rearrange("p j (m t) -> p m j t", t=TILES)
-            nc.vector.tensor_copy(dst[:, :VECTOR_SETS], src[:, :VECTOR_SETS])
-            nc.scalar.activation(dst[:, VECTOR_SETS:], src[:, VECTOR_SETS:], COPY)
+            nc.vector.tensor_scalar(dst[:, :VECTOR_SETS], src[:, :VECTOR_SETS], -1.0, None, ALU.mult)
+            nc.scalar.activation(dst[:, VECTOR_SETS:], src[:, VECTOR_SETS:], COPY, scale=-1.0)
+
+        def quantise_w(g):
             nc.vector.quantize_mx(
                 out=w_codes[g][:].bitcast(FP8X4),
                 scales=w_scales[g][:],
@@ -90,30 +97,51 @@ def tile_picked_clipsgd_none_p_kernel(tc, x_words, x_scales, w1, par, offs, ent,
         nc.vector.tensor_copy(picked[:], xs_all[:].indirect(offs_sb[:]))
         for g in range(PASSES):
             nc.vector.tensor_copy(x_scale[g][:].bitcast(I32), picked[:].bitcast(I32))
+        kept_rows = keep.tile([P, H], U8, name="kept_rows", align_bytes=ALIGN)
+        nc.vector.tensor_copy(kept_rows[:].bitcast(I32), picked[:, second].bitcast(I32))
 
-        def move_scale_rows(g):
-            for i in range(1, QUAD_ROWS):
-                nc.sync.dma_start(
-                    out=x_scale[g][QUAD_ROWS * g + i : P : QUAD, :].bitcast(I32),
-                    in_=x_scale[1 - g][QUAD_ROWS * g + SPREAD * i : P : QUAD, :].bitcast(I32),
-                )
+        def move_scale_row(g, i, entries, source):
+            nc.sync.dma_start(
+                out=x_scale[g][QUAD_ROWS * g + i : P : QUAD, entries].bitcast(I32),
+                in_=source[QUAD_ROWS * g + SPREAD * i : P : QUAD, :].bitcast(I32),
+            )
 
-        move_scale_rows(0)
+        def late_copy(g):
+            rows = keep.tile([P, H], U8, name=f"late_rows{g}", tag=f"w_raw{g}", align_bytes=ALIGN)
+            nc.vector.tensor_copy(rows[:].bitcast(I32), kept_rows[:].bitcast(I32))
+            return rows
+
+        for i in range(1, QUAD_ROWS):
+            move_scale_row(0, i, slice(0, S), x_scale[1][:])
         x_all.append(keep.tile([P, T], U32, name="x_all1", tag="picked", align_bytes=ALIGN))
         load_x(1, slice(0, T))
-        move_scale_rows(1)
+        move_scale_row(1, 1, slice(0, S), x_scale[0][:])
+        for i in (2, 3):
+            move_scale_row(1, i, first, x_scale[0][:, first])
+        cast_w(0)
         quantise_w(0)
+        late_rows = [late_copy(0)]
         nc.vector.tensor_copy(x_codes[0][:], x_all[0][:].indirect(offs_sb[:]))
+        cast_w(1)
+        late_rows.append(late_copy(1))
         quantise_w(1)
 
-        table = [keep.tile([P, U], F32, name=f"table{t}", tag=tag, align_bytes=ALIGN) for t, tag in enumerate(("w_bf0", "x_all0", "w_raw1"))]
-        for t in range(3):
+        table = [keep.tile([P, U], F32, name="table0", tag="w_bf0", align_bytes=ALIGN)]
+        table.extend(laid.tile([P, U], F32, name=f"table{t}", align_bytes=ALIGN, offset=(t - 1) * U * 4) for t in (1, 2))
+        table.append(keep.tile([P, U], F32, name="table3", tag="w_bf1", align_bytes=ALIGN))
+
+        def load_par(t):
             nc.sync.dma_start(out=table[t][:], in_=par_rows[:, t, :])
 
-        halves = [slice(0, S // 2), slice(S // 2, S)]
-        first, second = halves
-        pieces = [(0, first), (1, first), (2, first), (0, second), (1, second), (3, first), (2, second), (3, second)]
-        acc = [psum.tile([P, entries.stop - entries.start], F32, name=f"acc{n}") for n, (t, entries) in enumerate(pieces)]
+        load_par(0)
+        move_scale_row(1, 2, second, late_rows[0][:])
+        load_par(1)
+        load_par(2)
+        move_scale_row(1, 3, second, late_rows[1][:])
+        load_par(3)
+
+        pieces = [(0, first), (1, first), (2, first), (1, second), (0, second), (3, first), (2, second), (3, second)]
+        acc = [psum.tile([P, H], F32, name=f"acc{n}") for n in range(len(pieces))]
 
         def product(g, n):
             t, entries = pieces[n]
@@ -132,63 +160,50 @@ def tile_picked_clipsgd_none_p_kernel(tc, x_words, x_scales, w1, par, offs, ent,
             product(0, n)
         for entries in halves:
             nc.vector.tensor_copy(x_codes[1][:, entries], x_all[1][:].indirect(offs_sb[:, list_columns(entries)]))
-        for n in range(len(pieces)):
-            product(1, n)
+        for entries in halves:
+            for n in range(len(pieces)):
+                if pieces[n][1] == entries:
+                    product(1, n)
 
-        table.append(keep.tile([P, U], F32, name="table3", tag="w_bf1", align_bytes=ALIGN))
-        nc.sync.dma_start(out=table[3][:], in_=par_rows[:, 3, :])
-
-        H = S // 2
-        steps = [keep.tile([P, H], F32, name=f"step{n}") for n in range(3)]
-        y_sb = steps[2]
-        looked = [keep.tile([P, H], F32, name=f"looked{n}") for n in range(5)]
-        new = [keep.tile([P, S], F32, name=f"new{t}") for t in range(TILES)]
-        shrunk = [looked[n] for n in (0, 4, 1, 1, 2, 1, 3, 2)]
-        step = [steps[n] for n in (0, 1, 2, 0, 1, 0, 1, 0)]
+        step = [keep.tile([P, H], F32, name=f"step{n}") for n in range(len(pieces))]
+        y_first = keep.tile([P, H], F32, name="y_first", tag="w_raw0", align_bytes=ALIGN)
+        y_rest = keep.tile([P, H], F32, name="y_rest")
+        shrunk = [
+            keep.tile([P, H], F32, name=f"shrunk{n}", tag="w_raw1" if pieces[n] == (0, second) else f"shrunk{n}", align_bytes=ALIGN)
+            for n in range(len(pieces))
+        ]
 
         def look_up(n):
             t, entries = pieces[n]
             nc.scalar.activation(shrunk[n][:], table[t][:].indirect(ent_sb[:, list_columns(entries)]), COPY, scale=DECAY)
 
         def clip(n):
+            y_sb = y_first if n == VECTOR_CLIPS else y_rest
             nc.scalar.activation(y_sb[:], acc[n][:], COPY)
             nc.gpsimd.tensor_scalar(step[n][:], y_sb[:], CLIP, -CLIP, ALU.min, ALU.max)
 
-        def subtract(n, engine):
-            t, entries = pieces[n]
-            engine.tensor_tensor(new[t][:, entries], shrunk[n][:], step[n][:], ALU.subtract)
-
         def scatter(n):
             t, entries = pieces[n]
-            nc.vector.tensor_copy(table[t][:].indirect(ent_sb[:, list_columns(entries)]), new[t][:, entries])
-            if entries.stop == S:
+            nc.vector.tensor_tensor(table[t][:].indirect(ent_sb[:, list_columns(entries)]), shrunk[n][:], step[n][:], ALU.add)
+            if all(later != t for later, rest in pieces[n + 1 :]):
                 nc.sync.dma_start(out=out_rows[:, t, :], in_=table[t][:])
 
         look_up(0)
-        for n in range(3):
+        for n in range(VECTOR_CLIPS):
             nc.vector.tensor_scalar(step[n][:], acc[n][:], CLIP, -CLIP, ALU.min, ALU.max)
-        subtract(0, nc.vector)
         scatter(0)
+        clip(2)
         look_up(1)
-        look_up(4)
-        subtract(1, nc.gpsimd)
+        look_up(3)
         scatter(1)
         look_up(2)
         look_up(6)
-        subtract(2, nc.gpsimd)
         scatter(2)
         clip(3)
-        look_up(3)
-        clip(4)
-        subtract(3, nc.gpsimd)
+        look_up(4)
         scatter(3)
-        clip(5)
         look_up(5)
-        subtract(4, nc.gpsimd)
-        scatter(4)
         look_up(7)
-        for n in range(5, len(pieces)):
-            if n + 1 < len(pieces):
-                clip(n + 1)
-            subtract(n, nc.gpsimd)
+        for n in range(4, len(pieces)):
+            clip(n)
             scatter(n)

@@ -106,9 +106,8 @@ def tile_picked_clipsgd_none_p_kernel(tc, x_words, x_scales, w1, par, offs, ent,
                 in_=source[QUAD_ROWS * g + SPREAD * i : P : QUAD, :].bitcast(I32),
             )
 
-        def late_copy(g):
-            rows = keep.tile([P, H], U8, name=f"late_rows{g}", tag=f"w_raw{g}", align_bytes=ALIGN)
-            nc.vector.tensor_copy(rows[:].bitcast(I32), kept_rows[:].bitcast(I32))
+        def late_copy(rows):
+            nc.vector.tensor_copy(rows.bitcast(I32), kept_rows[:].bitcast(I32))
             return rows
 
         for i in range(1, QUAD_ROWS):
@@ -120,10 +119,10 @@ def tile_picked_clipsgd_none_p_kernel(tc, x_words, x_scales, w1, par, offs, ent,
             move_scale_row(1, i, first, x_scale[0][:, first])
         cast_w(0)
         quantise_w(0)
-        late_rows = [late_copy(0)]
+        late_rows = [late_copy(keep.tile([P, H], U8, name="late_rows0", tag="w_raw0", align_bytes=ALIGN)[:])]
         nc.vector.tensor_copy(x_codes[0][:], x_all[0][:].indirect(offs_sb[:]))
         cast_w(1)
-        late_rows.append(late_copy(1))
+        late_rows.append(late_copy(keep.tile([P, H], U8, name="late_rows1", tag="w_raw1", align_bytes=ALIGN)[:]))
         quantise_w(1)
 
         table = [keep.tile([P, U], F32, name="table0", tag="w_bf0", align_bytes=ALIGN)]
@@ -134,14 +133,15 @@ def tile_picked_clipsgd_none_p_kernel(tc, x_words, x_scales, w1, par, offs, ent,
             nc.sync.dma_start(out=table[t][:], in_=par_rows[:, t, :])
 
         load_par(0)
-        move_scale_row(1, 2, second, late_rows[0][:])
+        move_scale_row(1, 2, second, late_rows[0])
         load_par(1)
         load_par(2)
-        move_scale_row(1, 3, second, late_rows[1][:])
+        move_scale_row(1, 3, second, late_rows[1])
         load_par(3)
 
-        pieces = [(0, first), (1, first), (2, first), (1, second), (0, second), (3, first), (2, second), (3, second)]
-        acc = [psum.tile([P, H], F32, name=f"acc{n}") for n in range(len(pieces))]
+        pieces = [(0, first), (1, first), (2, first), (0, second), (2, second), (1, second), (3, slice(0, S))]
+        width = [entries.stop - entries.start for t, entries in pieces]
+        acc = [psum.tile([P, width[n]], F32, name=f"acc{n}") for n in range(len(pieces))]
 
         def product(g, n):
             t, entries = pieces[n]
@@ -160,27 +160,28 @@ def tile_picked_clipsgd_none_p_kernel(tc, x_words, x_scales, w1, par, offs, ent,
             product(0, n)
         for entries in halves:
             nc.vector.tensor_copy(x_codes[1][:, entries], x_all[1][:].indirect(offs_sb[:, list_columns(entries)]))
-        for entries in halves:
-            for n in range(len(pieces)):
-                if pieces[n][1] == entries:
-                    product(1, n)
+        for n in range(len(pieces)):
+            product(1, n)
 
-        step = [keep.tile([P, H], F32, name=f"step{n}") for n in range(len(pieces))]
+        step = [keep.tile([P, width[n]], F32, name=f"step{n}") for n in range(len(pieces))]
         y_first = keep.tile([P, H], F32, name="y_first", tag="w_raw0", align_bytes=ALIGN)
-        y_rest = keep.tile([P, H], F32, name="y_rest")
-        shrunk = [
-            keep.tile([P, H], F32, name=f"shrunk{n}", tag="w_raw1" if pieces[n] == (0, second) else f"shrunk{n}", align_bytes=ALIGN)
-            for n in range(len(pieces))
-        ]
+        y_rest = [keep.tile([P, S], F32, name=f"y_rest{n}") for n in range(2)]
+        shrunk = []
+        for n in range(len(pieces)):
+            if n == 5:
+                shrunk.append(shrunk[2])
+            else:
+                tag = "w_raw1" if n == 3 else f"shrunk{n}"
+                shrunk.append(keep.tile([P, width[n]], F32, name=f"shrunk{n}", tag=tag, align_bytes=ALIGN))
 
         def look_up(n):
             t, entries = pieces[n]
             nc.scalar.activation(shrunk[n][:], table[t][:].indirect(ent_sb[:, list_columns(entries)]), COPY, scale=DECAY)
 
         def clip(n):
-            y_sb = y_first if n == VECTOR_CLIPS else y_rest
-            nc.scalar.activation(y_sb[:], acc[n][:], COPY)
-            nc.gpsimd.tensor_scalar(step[n][:], y_sb[:], CLIP, -CLIP, ALU.min, ALU.max)
+            y_sb = y_first[:] if n == VECTOR_CLIPS else y_rest[n % 2][:, : width[n]]
+            nc.scalar.activation(y_sb, acc[n][:], COPY)
+            nc.gpsimd.tensor_scalar(step[n][:], y_sb, CLIP, -CLIP, ALU.min, ALU.max)
 
         def scatter(n):
             t, entries = pieces[n]
@@ -194,16 +195,15 @@ def tile_picked_clipsgd_none_p_kernel(tc, x_words, x_scales, w1, par, offs, ent,
         scatter(0)
         clip(2)
         look_up(1)
-        look_up(3)
         scatter(1)
         look_up(2)
-        look_up(6)
+        look_up(4)
         scatter(2)
         clip(3)
-        look_up(4)
+        look_up(3)
         scatter(3)
         look_up(5)
-        look_up(7)
+        look_up(6)
         for n in range(4, len(pieces)):
             clip(n)
             scatter(n)

@@ -163,47 +163,43 @@ def tile_picked_clipsgd_none_p_kernel(tc, x_words, x_scales, w1, par, offs, ent,
         for n in range(len(pieces)):
             product(1, n)
 
-        step = [keep.tile([P, width[n]], F32, name=f"step{n}") for n in range(len(pieces))]
+        steps = [keep.tile([P, S], F32, name=f"step{n}") for n in range(2)]
+        step = [steps[n % 2][:, : width[n]] for n in range(len(pieces))]
         y_first = keep.tile([P, H], F32, name="y_first", tag="w_raw0", align_bytes=ALIGN)
         y_rest = [keep.tile([P, S], F32, name=f"y_rest{n}") for n in range(2)]
-        shrunk = []
-        for n in range(len(pieces)):
-            if n == 5:
-                shrunk.append(shrunk[2])
-            else:
-                tag = "w_raw1" if n == 3 else f"shrunk{n}"
-                shrunk.append(keep.tile([P, width[n]], F32, name=f"shrunk{n}", tag=tag, align_bytes=ALIGN))
+        looked = [keep.tile([P, H], F32, name=f"looked{t}") for t in range(2)]
+        looked.extend(keep.tile([P, S], F32, name=f"looked{t}") for t in range(2, TILES))
+        held = keep.tile([P, H], F32, name="held", tag="w_raw1", align_bytes=ALIGN)
+        shrunk = [looked[0][:], looked[1][:], looked[2][:, first], held[:], looked[2][:, second], looked[2][:, first], looked[3][:]]
 
-        def look_up(n):
-            t, entries = pieces[n]
-            nc.scalar.activation(shrunk[n][:], table[t][:].indirect(ent_sb[:, list_columns(entries)]), COPY, scale=DECAY)
+        def look_up(t, entries, into):
+            nc.scalar.activation(into, table[t][:].indirect(ent_sb[:, list_columns(entries)]), COPY, scale=DECAY)
 
         def clip(n):
             y_sb = y_first[:] if n == VECTOR_CLIPS else y_rest[n % 2][:, : width[n]]
             nc.scalar.activation(y_sb, acc[n][:], COPY)
-            nc.gpsimd.tensor_scalar(step[n][:], y_sb, CLIP, -CLIP, ALU.min, ALU.max)
+            nc.gpsimd.tensor_scalar(step[n], y_sb, CLIP, -CLIP, ALU.min, ALU.max)
 
         def scatter(n):
             t, entries = pieces[n]
-            nc.vector.tensor_tensor(table[t][:].indirect(ent_sb[:, list_columns(entries)]), shrunk[n][:], step[n][:], ALU.add)
+            nc.vector.tensor_tensor(table[t][:].indirect(ent_sb[:, list_columns(entries)]), shrunk[n], step[n], ALU.add)
             if all(later != t for later, rest in pieces[n + 1 :]):
                 nc.sync.dma_start(out=out_rows[:, t, :], in_=table[t][:])
 
-        look_up(0)
+        look_up(0, first, shrunk[0])
         for n in range(VECTOR_CLIPS):
-            nc.vector.tensor_scalar(step[n][:], acc[n][:], CLIP, -CLIP, ALU.min, ALU.max)
+            nc.vector.tensor_scalar(step[n], acc[n][:], CLIP, -CLIP, ALU.min, ALU.max)
         scatter(0)
         clip(2)
-        look_up(1)
+        look_up(1, first, shrunk[1])
         scatter(1)
-        look_up(2)
-        look_up(4)
+        look_up(2, slice(0, S), looked[2][:])
         scatter(2)
         clip(3)
-        look_up(3)
+        look_up(0, second, shrunk[3])
         scatter(3)
-        look_up(5)
-        look_up(6)
+        look_up(1, second, shrunk[5])
+        look_up(3, slice(0, S), shrunk[6])
         for n in range(4, len(pieces)):
             clip(n)
             scatter(n)

@@ -26,7 +26,6 @@ SPREAD = QUAD // QUAD_ROWS
 GROUP = 16
 DECAY = 0.875
 CLIP = 0.75
-VECTOR_SETS = 80
 VECTOR_CLIPS = 2
 ALIGN = 256
 H = S // 2
@@ -45,7 +44,7 @@ def tile_picked_clipsgd_none_p_kernel(tc, x_words, x_scales, w1, par, offs, ent,
         offs_sb = keep.tile([P, S // GROUP], U16, name="offs_sb", align_bytes=ALIGN)
         ent_sb = keep.tile([P, S // GROUP], U16, name="ent_sb", align_bytes=ALIGN)
         w_raw = [keep.tile([P, PACK, N], F32, name=f"w_raw{g}", tag=f"w_raw{g}", align_bytes=ALIGN) for g in range(PASSES)]
-        x_all = [laid.tile([P, T], U32, name="x_all0", align_bytes=ALIGN, offset=0)]
+        x_all = [keep.tile([P, T], U32, name="x_all0", align_bytes=ALIGN)]
         xs_all = keep.tile([P, T], U8, name="xs_all", align_bytes=ALIGN)
 
         def load_w(g):
@@ -80,24 +79,28 @@ def tile_picked_clipsgd_none_p_kernel(tc, x_words, x_scales, w1, par, offs, ent,
         halves = [slice(0, H), slice(H, S)]
         first, second = halves
 
+        tile_pairs = [slice(0, 2), slice(2, TILES)]
+
         def cast_w(g):
             dst = w_bf[g][:].rearrange("p t m j -> p m j t")
             src = w_raw[g][:].rearrange("p j (m t) -> p m j t", t=TILES)
-            nc.vector.tensor_scalar(dst[:, :VECTOR_SETS], src[:, :VECTOR_SETS], -1.0, None, ALU.mult)
-            nc.scalar.activation(dst[:, VECTOR_SETS:], src[:, VECTOR_SETS:], COPY, scale=-1.0)
+            early, late = tile_pairs
+            nc.vector.tensor_scalar(dst[:, :, :, early], src[:, :, :, early], -1.0, None, ALU.mult)
+            nc.scalar.activation(dst[:, :, :, late], src[:, :, :, late], COPY, scale=-1.0)
 
-        def quantise_w(g):
+        def quantise_w(g, pair):
+            features = slice(pair.start * P, pair.stop * P)
             nc.vector.quantize_mx(
-                out=w_codes[g][:].bitcast(FP8X4),
-                scales=w_scales[g][:],
-                in_=w_bf[g][:].rearrange("p t m j -> p (t m j)"),
+                out=w_codes[g][:, features].bitcast(FP8X4),
+                scales=w_scales[g][:, features],
+                in_=w_bf[g][:, pair].rearrange("p t m j -> p (t m j)"),
             )
 
         picked = keep.tile([P, S], U8, name="picked", tag="picked", align_bytes=ALIGN)
         nc.vector.tensor_copy(picked[:], xs_all[:].indirect(offs_sb[:]))
         for g in range(PASSES):
             nc.vector.tensor_copy(x_scale[g][:].bitcast(I32), picked[:].bitcast(I32))
-        kept_rows = keep.tile([P, H], U8, name="kept_rows", align_bytes=ALIGN)
+        kept_rows = laid.tile([P, H], U8, name="kept_rows", align_bytes=H // 2, offset=U * 4 - H // 2)
         nc.vector.tensor_copy(kept_rows[:].bitcast(I32), picked[:, second].bitcast(I32))
 
         def move_scale_row(g, i, entries, source):
@@ -106,8 +109,8 @@ def tile_picked_clipsgd_none_p_kernel(tc, x_words, x_scales, w1, par, offs, ent,
                 in_=source[QUAD_ROWS * g + SPREAD * i : P : QUAD, :].bitcast(I32),
             )
 
-        def late_copy(rows):
-            nc.vector.tensor_copy(rows.bitcast(I32), kept_rows[:].bitcast(I32))
+        def late_copy(rows, source):
+            nc.vector.tensor_copy(rows.bitcast(I32), source.bitcast(I32))
             return rows
 
         for i in range(1, QUAD_ROWS):
@@ -118,14 +121,16 @@ def tile_picked_clipsgd_none_p_kernel(tc, x_words, x_scales, w1, par, offs, ent,
         for i in (2, 3):
             move_scale_row(1, i, first, x_scale[0][:, first])
         cast_w(0)
-        quantise_w(0)
-        late_rows = [late_copy(keep.tile([P, H], U8, name="late_rows0", tag="w_raw0", align_bytes=ALIGN)[:])]
+        for pair in tile_pairs:
+            quantise_w(0, pair)
+        late_rows = [late_copy(keep.tile([P, H], U8, name="late_rows0", tag="w_bf0", align_bytes=ALIGN)[:], kept_rows[:])]
         nc.vector.tensor_copy(x_codes[0][:], x_all[0][:].indirect(offs_sb[:]))
         cast_w(1)
-        late_rows.append(late_copy(keep.tile([P, H], U8, name="late_rows1", tag="w_raw1", align_bytes=ALIGN)[:]))
-        quantise_w(1)
+        quantise_w(1, tile_pairs[0])
+        late_rows.append(late_copy(keep.tile([P, H], U8, name="late_rows1", tag="w_raw1", align_bytes=ALIGN)[:], late_rows[0]))
+        quantise_w(1, tile_pairs[1])
 
-        table = [keep.tile([P, U], F32, name="table0", tag="w_bf0", align_bytes=ALIGN)]
+        table = [keep.tile([P, U], F32, name="table0", tag="w_raw0", align_bytes=ALIGN)]
         table.extend(laid.tile([P, U], F32, name=f"table{t}", align_bytes=ALIGN, offset=(t - 1) * U * 4) for t in (1, 2))
         table.append(keep.tile([P, U], F32, name="table3", tag="w_bf1", align_bytes=ALIGN))
 
@@ -165,7 +170,7 @@ def tile_picked_clipsgd_none_p_kernel(tc, x_words, x_scales, w1, par, offs, ent,
 
         steps = [keep.tile([P, S], F32, name=f"step{n}") for n in range(2)]
         step = [steps[n % 2][:, : width[n]] for n in range(len(pieces))]
-        y_first = keep.tile([P, H], F32, name="y_first", tag="w_raw0", align_bytes=ALIGN)
+        y_first = keep.tile([P, H], F32, name="y_first", tag="w_bf0", align_bytes=ALIGN)
         y_rest = [keep.tile([P, S], F32, name=f"y_rest{n}") for n in range(2)]
         looked = [keep.tile([P, H], F32, name=f"looked{t}") for t in range(2)]
         looked.extend(keep.tile([P, S], F32, name=f"looked{t}") for t in range(2, TILES))

@@ -29,6 +29,7 @@ CLIP = 0.75
 VECTOR_CLIPS = 2
 ALIGN = 256
 H = S // 2
+X1_AT = 2 * U * 4
 
 
 def tile_picked_clipsgd_none_p_kernel(tc, x_words, x_scales, w1, par, offs, ent, out):
@@ -62,20 +63,22 @@ def tile_picked_clipsgd_none_p_kernel(tc, x_words, x_scales, w1, par, offs, ent,
 
         nc.gpsimd.memset(xs_all[:].bitcast(I32), 0)
 
-        load_x(0, slice(0, T // 2))
+        load_x(0, slice(0, T))
         for g in range(PASSES):
             nc.sync.dma_start(out=xs_all[QUAD_ROWS * g : P : SPREAD, :].bitcast(I32), in_=x_scales[g].bitcast(I32))
         nc.sync.dma_start(offs_sb[:], offs)
         nc.sync.dma_start(ent_sb[:], ent)
         load_w(0)
-        load_x(0, slice(T // 2, T))
         load_w(1)
 
         x_scale = [keep.tile([P, S], U8, name=f"x_scale{g}", align_bytes=ALIGN) for g in range(PASSES)]
         w_bf = [keep.tile([P, TILES, P, PACK], BF16, name=f"w_bf{g}", tag=f"w_bf{g}", align_bytes=ALIGN) for g in range(PASSES)]
         w_codes = [keep.tile([P, N], U32, name=f"w_codes{g}", align_bytes=ALIGN) for g in range(PASSES)]
         w_scales = [keep.tile([P, N], U8, name=f"w_scales{g}", align_bytes=ALIGN) for g in range(PASSES)]
-        x_codes = [keep.tile([P, S], U32, name=f"x_codes{g}", align_bytes=ALIGN) for g in range(PASSES)]
+        x_codes = [
+            laid.tile([P, S], U32, name="x_codes0", align_bytes=ALIGN, offset=X1_AT + T * 4),
+            keep.tile([P, S], U32, name="x_codes1", align_bytes=ALIGN),
+        ]
         halves = [slice(0, H), slice(H, S)]
         first, second = halves
 
@@ -96,7 +99,7 @@ def tile_picked_clipsgd_none_p_kernel(tc, x_words, x_scales, w1, par, offs, ent,
                 in_=w_bf[g][:, pair].rearrange("p t m j -> p (t m j)"),
             )
 
-        picked = keep.tile([P, S], U8, name="picked", tag="picked", align_bytes=ALIGN)
+        picked = laid.tile([P, S], U8, name="picked", align_bytes=ALIGN, offset=X1_AT + T * 4 - H)
         nc.vector.tensor_copy(picked[:], xs_all[:].indirect(offs_sb[:]))
         for g in range(PASSES):
             nc.vector.tensor_copy(x_scale[g][:].bitcast(I32), picked[:].bitcast(I32))
@@ -115,7 +118,7 @@ def tile_picked_clipsgd_none_p_kernel(tc, x_words, x_scales, w1, par, offs, ent,
 
         for i in range(1, QUAD_ROWS):
             move_scale_row(0, i, slice(0, S), x_scale[1][:])
-        x_all.append(keep.tile([P, T], U32, name="x_all1", tag="picked", align_bytes=ALIGN))
+        x_all.append(laid.tile([P, T], U32, name="x_all1", align_bytes=ALIGN, offset=X1_AT))
         load_x(1, slice(0, T))
         move_scale_row(1, 1, slice(0, S), x_scale[0][:])
         for i in (2, 3):

@@ -61,7 +61,7 @@ def tile_picked_clipsgd_none_p_kernel(tc, x_words, x_scales, w1, par, offs, ent,
         def list_columns(entries):
             return slice(entries.start // GROUP, entries.stop // GROUP)
 
-        nc.gpsimd.memset(xs_all[:].bitcast(I32), 0)
+        nc.vector.memset(xs_all[:].bitcast(I32), 0)
 
         load_x(0, slice(0, T))
         for g in range(PASSES):

@@ -67,9 +67,9 @@ def tile_picked_clipsgd_none_p_kernel(tc, x_words, x_scales, w1, par, offs, ent,
         for g in range(PASSES):
             nc.sync.dma_start(out=xs_all[QUAD_ROWS * g : P : SPREAD, :].bitcast(I32), in_=x_scales[g].bitcast(I32))
         nc.sync.dma_start(offs_sb[:], offs)
-        nc.sync.dma_start(ent_sb[:], ent)
         load_w(0)
         load_w(1)
+        nc.sync.dma_start(ent_sb[:], ent)
 
         x_scale = [keep.tile([P, S], U8, name=f"x_scale{g}", align_bytes=ALIGN) for g in range(PASSES)]
         w_bf = [keep.tile([P, TILES, P, PACK], BF16, name=f"w_bf{g}", tag=f"w_bf{g}", align_bytes=ALIGN) for g in range(PASSES)]

@@ -149,13 +149,16 @@ def tile_picked_clipsgd_none_p_kernel(tc, x_words, x_scales, w1, par, offs, ent,
 
         pieces = [(0, first), (1, first), (2, first), (0, second), (2, second), (1, second), (3, slice(0, S))]
         width = [entries.stop - entries.start for t, entries in pieces]
-        acc = [psum.tile([P, width[n]], F32, name=f"acc{n}") for n in range(len(pieces))]
+        quarters = [slice(0, H // 2), slice(H // 2, H)]
+        parts = [(0, entries) for entries in quarters] + [(n, pieces[n][1]) for n in range(1, len(pieces))]
+        bank = {(n, entries.start): psum.tile([P, entries.stop - entries.start], F32, name=f"acc{n}_{entries.start}") for n, entries in parts}
+        acc = [bank[n, pieces[n][1].start] for n in range(len(pieces))]
 
-        def product(g, n):
-            t, entries = pieces[n]
+        def product(g, n, entries):
+            t = pieces[n][0]
             features = slice(t * P, (t + 1) * P)
             nc.tensor.matmul_mx(
-                out=acc[n][:],
+                out=bank[n, entries.start][:],
                 lhsT=w_codes[g][:, features].bitcast(FP8X4),
                 lhsT_scale=w_scales[g][:, features],
                 rhs=x_codes[g][:, entries].bitcast(FP8X4),
@@ -164,12 +167,12 @@ def tile_picked_clipsgd_none_p_kernel(tc, x_words, x_scales, w1, par, offs, ent,
                 stop=(g == PASSES - 1),
             )
 
-        for n in range(len(pieces)):
-            product(0, n)
-        for entries in halves:
+        for n, entries in parts:
+            product(0, n, entries)
+        for entries in quarters + [second]:
             nc.vector.tensor_copy(x_codes[1][:, entries], x_all[1][:].indirect(offs_sb[:, list_columns(entries)]))
-        for n in range(len(pieces)):
-            product(1, n)
+        for n, entries in parts:
+            product(1, n, entries)
 
         steps = [keep.tile([P, S], F32, name=f"step{n}") for n in range(2)]
         step = [steps[n % 2][:, : width[n]] for n in range(len(pieces))]
@@ -195,8 +198,8 @@ def tile_picked_clipsgd_none_p_kernel(tc, x_words, x_scales, w1, par, offs, ent,
                 nc.sync.dma_start(out=out_rows[:, t, :], in_=table[t][:])
 
         look_up(0, first, shrunk[0])
-        for n in range(VECTOR_CLIPS):
-            nc.vector.tensor_scalar(step[n], acc[n][:], CLIP, -CLIP, ALU.min, ALU.max)
+        for n, entries in parts[: VECTOR_CLIPS + 1]:
+            nc.vector.tensor_scalar(step[n][:, entries], bank[n, entries.start][:], CLIP, -CLIP, ALU.min, ALU.max)
         scatter(0)
         clip(2)
         look_up(1, first, shrunk[1])

@@ -20,16 +20,18 @@ PACK = 4
 K_PASS = P * PACK
 PASSES = K // K_PASS
 TILES = N // P
+PAIR = 2
 QUAD = 32
 QUAD_ROWS = 4
 SPREAD = QUAD // QUAD_ROWS
 GROUP = 16
 DECAY = 0.875
 CLIP = 0.75
-VECTOR_CLIPS = 2
 ALIGN = 256
 H = S // 2
-X1_AT = 2 * U * 4
+W_BYTES = PACK * N * 4
+W_STEP = W_BYTES + H * 4
+X1_AT = PASSES * W_STEP
 
 
 def tile_picked_clipsgd_none_p_kernel(tc, x_words, x_scales, w1, par, offs, ent, out):
@@ -44,7 +46,7 @@ def tile_picked_clipsgd_none_p_kernel(tc, x_words, x_scales, w1, par, offs, ent,
 
         offs_sb = keep.tile([P, S // GROUP], U16, name="offs_sb", align_bytes=ALIGN)
         ent_sb = keep.tile([P, S // GROUP], U16, name="ent_sb", align_bytes=ALIGN)
-        w_raw = [keep.tile([P, PACK, N], F32, name=f"w_raw{g}", tag=f"w_raw{g}", align_bytes=ALIGN) for g in range(PASSES)]
+        w_raw = [laid.tile([P, PACK, N], F32, name=f"w_raw{g}", align_bytes=ALIGN, offset=g * W_STEP) for g in range(PASSES)]
         x_all = [keep.tile([P, T], U32, name="x_all0", align_bytes=ALIGN)]
         xs_all = keep.tile([P, T], U8, name="xs_all", align_bytes=ALIGN)
 
@@ -52,18 +54,15 @@ def tile_picked_clipsgd_none_p_kernel(tc, x_words, x_scales, w1, par, offs, ent,
             rows = w1[g * K_PASS : (g + 1) * K_PASS, :]
             nc.sync.dma_start(out=w_raw[g][:], in_=rows.rearrange("(p j) c -> p j c", j=PACK))
 
-        def load_x(g, columns):
-            nc.sync.dma_start(
-                out=x_all[g][:].bitcast(I32)[:, columns],
-                in_=x_words[g].rearrange("p n r -> p (n r)").bitcast(I32)[:, columns],
-            )
+        def load_x(g):
+            nc.sync.dma_start(out=x_all[g][:].bitcast(I32), in_=x_words[g].rearrange("p n r -> p (n r)").bitcast(I32))
 
         def list_columns(entries):
             return slice(entries.start // GROUP, entries.stop // GROUP)
 
         nc.vector.memset(xs_all[:].bitcast(I32), 0)
 
-        load_x(0, slice(0, T))
+        load_x(0)
         for g in range(PASSES):
             nc.sync.dma_start(out=xs_all[QUAD_ROWS * g : P : SPREAD, :].bitcast(I32), in_=x_scales[g].bitcast(I32))
         nc.sync.dma_start(offs_sb[:], offs)
@@ -72,17 +71,16 @@ def tile_picked_clipsgd_none_p_kernel(tc, x_words, x_scales, w1, par, offs, ent,
         nc.sync.dma_start(ent_sb[:], ent)
 
         x_scale = [keep.tile([P, S], U8, name=f"x_scale{g}", align_bytes=ALIGN) for g in range(PASSES)]
-        w_bf = [keep.tile([P, TILES, P, PACK], BF16, name=f"w_bf{g}", tag=f"w_bf{g}", align_bytes=ALIGN) for g in range(PASSES)]
+        w_bf = [keep.tile([P, TILES, P, PACK], BF16, name=f"w_bf{g}", align_bytes=ALIGN) for g in range(PASSES)]
         w_codes = [keep.tile([P, N], U32, name=f"w_codes{g}", align_bytes=ALIGN) for g in range(PASSES)]
         w_scales = [keep.tile([P, N], U8, name=f"w_scales{g}", align_bytes=ALIGN) for g in range(PASSES)]
         x_codes = [
             laid.tile([P, S], U32, name="x_codes0", align_bytes=ALIGN, offset=X1_AT + T * 4),
             keep.tile([P, S], U32, name="x_codes1", align_bytes=ALIGN),
         ]
+        whole = slice(0, S)
         halves = [slice(0, H), slice(H, S)]
-        first, second = halves
-
-        tile_pairs = [slice(0, 2), slice(2, TILES)]
+        tile_pairs = [slice(0, PAIR), slice(PAIR, TILES)]
 
         def cast_w(g):
             dst = w_bf[g][:].rearrange("p t m j -> p m j t")
@@ -91,126 +89,96 @@ def tile_picked_clipsgd_none_p_kernel(tc, x_words, x_scales, w1, par, offs, ent,
             nc.vector.tensor_scalar(dst[:, :, :, early], src[:, :, :, early], -1.0, None, ALU.mult)
             nc.scalar.activation(dst[:, :, :, late], src[:, :, :, late], COPY, scale=-1.0)
 
-        def quantise_w(g, pair):
-            features = slice(pair.start * P, pair.stop * P)
-            nc.vector.quantize_mx(
-                out=w_codes[g][:, features].bitcast(FP8X4),
-                scales=w_scales[g][:, features],
-                in_=w_bf[g][:, pair].rearrange("p t m j -> p (t m j)"),
-            )
+        def quantise_w(g):
+            for pair in tile_pairs:
+                features = slice(pair.start * P, pair.stop * P)
+                nc.vector.quantize_mx(
+                    out=w_codes[g][:, features].bitcast(FP8X4),
+                    scales=w_scales[g][:, features],
+                    in_=w_bf[g][:, pair].rearrange("p t m j -> p (t m j)"),
+                )
 
         picked = laid.tile([P, S], U8, name="picked", align_bytes=ALIGN, offset=X1_AT + T * 4 - H)
         nc.vector.tensor_copy(picked[:], xs_all[:].indirect(offs_sb[:]))
         for g in range(PASSES):
             nc.vector.tensor_copy(x_scale[g][:].bitcast(I32), picked[:].bitcast(I32))
-        kept_rows = laid.tile([P, H], U8, name="kept_rows", align_bytes=H // 2, offset=U * 4 - H // 2)
-        nc.vector.tensor_copy(kept_rows[:].bitcast(I32), picked[:, second].bitcast(I32))
 
-        def move_scale_row(g, i, entries, source):
-            nc.sync.dma_start(
-                out=x_scale[g][QUAD_ROWS * g + i : P : QUAD, entries].bitcast(I32),
-                in_=source[QUAD_ROWS * g + SPREAD * i : P : QUAD, :].bitcast(I32),
-            )
+        def move_scale_rows(g):
+            for i in range(1, QUAD_ROWS):
+                nc.sync.dma_start(
+                    out=x_scale[g][QUAD_ROWS * g + i : P : QUAD, :].bitcast(I32),
+                    in_=x_scale[1 - g][QUAD_ROWS * g + SPREAD * i : P : QUAD, :].bitcast(I32),
+                )
 
-        def late_copy(rows, source):
-            nc.vector.tensor_copy(rows.bitcast(I32), source.bitcast(I32))
-            return rows
-
-        for i in range(1, QUAD_ROWS):
-            move_scale_row(0, i, slice(0, S), x_scale[1][:])
+        move_scale_rows(0)
         x_all.append(laid.tile([P, T], U32, name="x_all1", align_bytes=ALIGN, offset=X1_AT))
-        load_x(1, slice(0, T))
-        move_scale_row(1, 1, slice(0, S), x_scale[0][:])
-        for i in (2, 3):
-            move_scale_row(1, i, first, x_scale[0][:, first])
+        load_x(1)
+        move_scale_rows(1)
         cast_w(0)
-        for pair in tile_pairs:
-            quantise_w(0, pair)
-        late_rows = [late_copy(keep.tile([P, H], U8, name="late_rows0", tag="w_bf0", align_bytes=ALIGN)[:], kept_rows[:])]
+        quantise_w(0)
         nc.vector.tensor_copy(x_codes[0][:], x_all[0][:].indirect(offs_sb[:]))
         cast_w(1)
-        quantise_w(1, tile_pairs[0])
-        late_rows.append(late_copy(keep.tile([P, H], U8, name="late_rows1", tag="w_raw1", align_bytes=ALIGN)[:], late_rows[0]))
-        quantise_w(1, tile_pairs[1])
+        quantise_w(1)
 
-        table = [keep.tile([P, U], F32, name="table0", tag="w_raw0", align_bytes=ALIGN)]
-        table.extend(laid.tile([P, U], F32, name=f"table{t}", align_bytes=ALIGN, offset=(t - 1) * U * 4) for t in (1, 2))
-        table.append(keep.tile([P, U], F32, name="table3", tag="w_bf1", align_bytes=ALIGN))
+        table_at = [0, W_BYTES - U * 4, W_STEP + W_BYTES - U * 4, W_STEP]
+        table = [
+            laid.tile([P, U + (H if t in (1, 2) else 0)], F32, name=f"table{t}", align_bytes=ALIGN, offset=table_at[t])
+            for t in range(TILES)
+        ]
+        for t in range(TILES):
+            nc.sync.dma_start(out=table[t][:, :U], in_=par_rows[:, t, :])
 
-        def load_par(t):
-            nc.sync.dma_start(out=table[t][:], in_=par_rows[:, t, :])
+        bank = [[psum.tile([P, PAIR, H], F32, name=f"bank{h}_{n}") for n in range(2)] for h in range(2)]
 
-        load_par(0)
-        move_scale_row(1, 2, second, late_rows[0])
-        load_par(1)
-        load_par(2)
-        move_scale_row(1, 3, second, late_rows[1])
-        load_par(3)
+        def products(g, h):
+            for t in range(TILES):
+                features = slice(t * P, (t + 1) * P)
+                nc.tensor.matmul_mx(
+                    out=bank[h][t // PAIR][:, t % PAIR, :],
+                    lhsT=w_codes[g][:, features].bitcast(FP8X4),
+                    lhsT_scale=w_scales[g][:, features],
+                    rhs=x_codes[g][:, halves[h]].bitcast(FP8X4),
+                    rhs_scale=x_scale[g][QUAD_ROWS * g : P, halves[h]],
+                    start=(g == 0 and t % PAIR == 0),
+                    stop=(g == PASSES - 1 and t % PAIR == PAIR - 1),
+                )
 
-        pieces = [(0, first), (1, first), (2, first), (0, second), (2, second), (1, second), (3, slice(0, S))]
-        width = [entries.stop - entries.start for t, entries in pieces]
-        quarters = [slice(0, H // 2), slice(H // 2, H)]
-        parts = [(0, entries) for entries in quarters] + [(n, pieces[n][1]) for n in range(1, len(pieces))]
-        bank = {(n, entries.start): psum.tile([P, entries.stop - entries.start], F32, name=f"acc{n}_{entries.start}") for n, entries in parts}
-        acc = [bank[n, pieces[n][1].start] for n in range(len(pieces))]
-
-        def product(g, n, entries):
-            t = pieces[n][0]
-            features = slice(t * P, (t + 1) * P)
-            nc.tensor.matmul_mx(
-                out=bank[n, entries.start][:],
-                lhsT=w_codes[g][:, features].bitcast(FP8X4),
-                lhsT_scale=w_scales[g][:, features],
-                rhs=x_codes[g][:, entries].bitcast(FP8X4),
-                rhs_scale=x_scale[g][QUAD_ROWS * g : P, entries],
-                start=(g == 0),
-                stop=(g == PASSES - 1),
-            )
-
-        for n, entries in parts:
-            product(0, n, entries)
-        for entries in quarters + [second]:
+        for h in range(2):
+            products(0, h)
+        for entries in halves:
             nc.vector.tensor_copy(x_codes[1][:, entries], x_all[1][:].indirect(offs_sb[:, list_columns(entries)]))
-        for n, entries in parts:
-            product(1, n, entries)
+        for h in range(2):
+            products(1, h)
 
-        steps = [keep.tile([P, S], F32, name=f"step{n}") for n in range(2)]
-        step = [steps[n % 2][:, : width[n]] for n in range(len(pieces))]
-        y_first = keep.tile([P, H], F32, name="y_first", tag="w_bf0", align_bytes=ALIGN)
-        y_rest = [keep.tile([P, S], F32, name=f"y_rest{n}") for n in range(2)]
-        looked = [keep.tile([P, H], F32, name=f"looked{t}") for t in range(2)]
-        looked.extend(keep.tile([P, S], F32, name=f"looked{t}") for t in range(2, TILES))
-        held = keep.tile([P, H], F32, name="held", tag="w_raw1", align_bytes=ALIGN)
-        shrunk = [looked[0][:], looked[1][:], looked[2][:, first], held[:], looked[2][:, second], looked[2][:, first], looked[3][:]]
+        step = [keep.tile([P, PAIR, S], F32, name=f"step{n}") for n in range(2)]
+        shrunk = [keep.tile([P, S], F32, name=f"shrunk{t}") for t in range(TILES - 1)]
+        shrunk_last = [table[2][:, U:], table[1][:, U:]]
+        fresh = {t: keep.tile([P, S], F32, name=f"fresh{t}") for t in (1, 2)}
 
-        def look_up(t, entries, into):
-            nc.scalar.activation(into, table[t][:].indirect(ent_sb[:, list_columns(entries)]), COPY, scale=DECAY)
+        for h in range(2):
+            for n in range(2):
+                nc.vector.tensor_scalar(step[n][:, :, halves[h]], bank[h][n][:], CLIP, -CLIP, ALU.min, ALU.max)
 
-        def clip(n):
-            y_sb = y_first[:] if n == VECTOR_CLIPS else y_rest[n % 2][:, : width[n]]
-            nc.scalar.activation(y_sb, acc[n][:], COPY)
-            nc.gpsimd.tensor_scalar(step[n], y_sb, CLIP, -CLIP, ALU.min, ALU.max)
+        def picked_of(t, entries):
+            return table[t][:].indirect(ent_sb[:, list_columns(entries)])
 
-        def scatter(n):
-            t, entries = pieces[n]
-            nc.vector.tensor_tensor(table[t][:].indirect(ent_sb[:, list_columns(entries)]), shrunk[n], step[n], ALU.add)
-            if all(later != t for later, rest in pieces[n + 1 :]):
-                nc.sync.dma_start(out=out_rows[:, t, :], in_=table[t][:])
+        def store(t):
+            nc.sync.dma_start(out=out_rows[:, t, :], in_=table[t][:, :U])
 
-        look_up(0, first, shrunk[0])
-        for n, entries in parts[: VECTOR_CLIPS + 1]:
-            nc.vector.tensor_scalar(step[n][:, entries], bank[n, entries.start][:], CLIP, -CLIP, ALU.min, ALU.max)
-        scatter(0)
-        clip(2)
-        look_up(1, first, shrunk[1])
-        scatter(1)
-        look_up(2, slice(0, S), looked[2][:])
-        scatter(2)
-        clip(3)
-        look_up(0, second, shrunk[3])
-        scatter(3)
-        look_up(1, second, shrunk[5])
-        look_up(3, slice(0, S), shrunk[6])
-        for n in range(4, len(pieces)):
-            clip(n)
-            scatter(n)
+        for t in range(TILES - 1):
+            nc.scalar.activation(shrunk[t][:], picked_of(t, whole), COPY, scale=DECAY)
+            if t in fresh:
+                nc.gpsimd.tensor_tensor(fresh[t][:], shrunk[t][:], step[t // PAIR][:, t % PAIR, :], ALU.add)
+        for h in range(2):
+            nc.scalar.activation(shrunk_last[h], picked_of(3, halves[h]), COPY, scale=DECAY)
+
+        nc.vector.tensor_tensor(picked_of(0, whole), shrunk[0][:], step[0][:, 0, :], ALU.add)
+        store(0)
+        nc.scalar.activation(picked_of(1, whole), fresh[1][:], COPY)
+        store(1)
+        for h in range(2):
+            nc.vector.tensor_tensor(picked_of(3, halves[h]), shrunk_last[h], step[1][:, 1, halves[h]], ALU.add)
+            if h == 0:
+                nc.scalar.activation(picked_of(2, whole), fresh[2][:], COPY)
+        store(3)
+        store(2)

@@ -152,7 +152,7 @@ def tile_picked_clipsgd_none_p_kernel(tc, x_words, x_scales, w1, par, offs, ent,
 
         step = [keep.tile([P, PAIR, S], F32, name=f"step{n}") for n in range(2)]
         shrunk = [keep.tile([P, S], F32, name=f"shrunk{t}") for t in range(TILES - 1)]
-        shrunk_last = [table[2][:, U:], table[1][:, U:]]
+        shrunk_last = [table[1][:, U:], table[2][:, U:]]
         fresh = {t: keep.tile([P, S], F32, name=f"fresh{t}") for t in (1, 2)}
 
         for h in range(2):
@@ -176,9 +176,9 @@ def tile_picked_clipsgd_none_p_kernel(tc, x_words, x_scales, w1, par, offs, ent,
         store(0)
         nc.scalar.activation(picked_of(1, whole), fresh[1][:], COPY)
         store(1)
-        for h in range(2):
+        for h in (1, 0):
             nc.vector.tensor_tensor(picked_of(3, halves[h]), shrunk_last[h], step[1][:, 1, halves[h]], ALU.add)
-            if h == 0:
+            if h == 1:
                 nc.scalar.activation(picked_of(2, whole), fresh[2][:], COPY)
         store(3)
         store(2)

@@ -153,10 +153,10 @@ def tile_picked_clipsgd_none_p_kernel(tc, x_words, x_scales, w1, par, offs, ent,
         step = [keep.tile([P, PAIR, S], F32, name=f"step{n}") for n in range(2)]
         shrunk = [keep.tile([P, S], F32, name=f"shrunk{t}") for t in range(TILES - 1)]
         shrunk_last = [table[1][:, U:], table[2][:, U:]]
-        fresh = {t: keep.tile([P, S], F32, name=f"fresh{t}") for t in (1, 2)}
+        fresh = {t: keep.tile([P, S], F32, name=f"fresh{t}") for t in range(TILES)}
 
-        for h in range(2):
-            for n in range(2):
+        for n in range(2):
+            for h in range(2):
                 nc.vector.tensor_scalar(step[n][:, :, halves[h]], bank[h][n][:], CLIP, -CLIP, ALU.min, ALU.max)
 
         def picked_of(t, entries):
@@ -165,20 +165,24 @@ def tile_picked_clipsgd_none_p_kernel(tc, x_words, x_scales, w1, par, offs, ent,
         def store(t):
             nc.sync.dma_start(out=out_rows[:, t, :], in_=table[t][:, :U])
 
+        def add(t, entries, looked):
+            nc.gpsimd.tensor_tensor(fresh[t][:, entries], looked, step[t // PAIR][:, t % PAIR, entries], ALU.add)
+
         for t in range(TILES - 1):
             nc.scalar.activation(shrunk[t][:], picked_of(t, whole), COPY, scale=DECAY)
-            if t in fresh:
-                nc.gpsimd.tensor_tensor(fresh[t][:], shrunk[t][:], step[t // PAIR][:, t % PAIR, :], ALU.add)
+            for entries in halves if t == 0 else [whole]:
+                add(t, entries, shrunk[t][:, entries])
         for h in range(2):
             nc.scalar.activation(shrunk_last[h], picked_of(3, halves[h]), COPY, scale=DECAY)
+        first, second = halves
+        add(3, second, shrunk_last[1])
 
-        nc.vector.tensor_tensor(picked_of(0, whole), shrunk[0][:], step[0][:, 0, :], ALU.add)
+        nc.vector.tensor_copy(picked_of(0, whole), fresh[0][:])
         store(0)
         nc.scalar.activation(picked_of(1, whole), fresh[1][:], COPY)
         store(1)
-        for h in (1, 0):
-            nc.vector.tensor_tensor(picked_of(3, halves[h]), shrunk_last[h], step[1][:, 1, halves[h]], ALU.add)
-            if h == 1:
-                nc.scalar.activation(picked_of(2, whole), fresh[2][:], COPY)
+        nc.vector.tensor_copy(picked_of(3, second), fresh[3][:, second])
+        nc.vector.tensor_tensor(picked_of(3, first), shrunk_last[0], step[1][:, 1, first], ALU.add)
         store(3)
+        nc.scalar.activation(picked_of(2, whole), fresh[2][:], COPY)
         store(2)

@@ -30,8 +30,8 @@ CLIP = 0.75
 ALIGN = 256
 H = S // 2
 W_BYTES = PACK * N * 4
-W_STEP = W_BYTES + H * 4
-X1_AT = PASSES * W_STEP
+SHARE = 96
+X1_AT = PASSES * W_BYTES
 
 
 def tile_picked_clipsgd_none_p_kernel(tc, x_words, x_scales, w1, par, offs, ent, out):
@@ -46,7 +46,7 @@ def tile_picked_clipsgd_none_p_kernel(tc, x_words, x_scales, w1, par, offs, ent,
 
         offs_sb = keep.tile([P, S // GROUP], U16, name="offs_sb", align_bytes=ALIGN)
         ent_sb = keep.tile([P, S // GROUP], U16, name="ent_sb", align_bytes=ALIGN)
-        w_raw = [laid.tile([P, PACK, N], F32, name=f"w_raw{g}", align_bytes=ALIGN, offset=g * W_STEP) for g in range(PASSES)]
+        w_raw = [laid.tile([P, PACK, N], F32, name=f"w_raw{g}", align_bytes=ALIGN, offset=g * W_BYTES) for g in range(PASSES)]
         x_all = [keep.tile([P, T], U32, name="x_all0", align_bytes=ALIGN)]
         xs_all = keep.tile([P, T], U8, name="xs_all", align_bytes=ALIGN)
 
@@ -120,69 +120,75 @@ def tile_picked_clipsgd_none_p_kernel(tc, x_words, x_scales, w1, par, offs, ent,
         cast_w(1)
         quantise_w(1)
 
-        table_at = [0, W_BYTES - U * 4, W_STEP + W_BYTES - U * 4, W_STEP]
-        table = [
-            laid.tile([P, U + (H if t in (1, 2) else 0)], F32, name=f"table{t}", align_bytes=ALIGN, offset=table_at[t])
-            for t in range(TILES)
-        ]
+        table = [laid.tile([P, U], F32, name=f"table{t}", align_bytes=ALIGN, offset=t * U * 4) for t in range(TILES)]
         for t in range(TILES):
-            nc.sync.dma_start(out=table[t][:, :U], in_=par_rows[:, t, :])
+            nc.sync.dma_start(out=table[t][:], in_=par_rows[:, t, :])
 
-        bank = [[psum.tile([P, PAIR, H], F32, name=f"bank{h}_{n}") for n in range(2)] for h in range(2)]
+        first, second = halves
+        groups = [((0, 1), first), ((0, 1), second), ((2, 3), first), ((2, 3), second)]
+        bank = [psum.tile([P, len(tiles), H], F32, name=f"bank{n}") for n, (tiles, entries) in enumerate(groups)]
 
-        def products(g, h):
-            for t in range(TILES):
-                features = slice(t * P, (t + 1) * P)
-                nc.tensor.matmul_mx(
-                    out=bank[h][t // PAIR][:, t % PAIR, :],
-                    lhsT=w_codes[g][:, features].bitcast(FP8X4),
-                    lhsT_scale=w_scales[g][:, features],
-                    rhs=x_codes[g][:, halves[h]].bitcast(FP8X4),
-                    rhs_scale=x_scale[g][QUAD_ROWS * g : P, halves[h]],
-                    start=(g == 0 and t % PAIR == 0),
-                    stop=(g == PASSES - 1 and t % PAIR == PAIR - 1),
-                )
+        def products(g):
+            for n, (tiles, entries) in enumerate(groups):
+                for i, t in enumerate(tiles):
+                    features = slice(t * P, (t + 1) * P)
+                    nc.tensor.matmul_mx(
+                        out=bank[n][:, i, :],
+                        lhsT=w_codes[g][:, features].bitcast(FP8X4),
+                        lhsT_scale=w_scales[g][:, features],
+                        rhs=x_codes[g][:, entries].bitcast(FP8X4),
+                        rhs_scale=x_scale[g][QUAD_ROWS * g : P, entries],
+                        start=(g == 0 and i == 0),
+                        stop=(g == PASSES - 1 and i == len(tiles) - 1),
+                    )
 
-        for h in range(2):
-            products(0, h)
+        products(0)
         for entries in halves:
             nc.vector.tensor_copy(x_codes[1][:, entries], x_all[1][:].indirect(offs_sb[:, list_columns(entries)]))
-        for h in range(2):
-            products(1, h)
+        products(1)
 
         step = [keep.tile([P, PAIR, S], F32, name=f"step{n}") for n in range(2)]
-        shrunk = [keep.tile([P, S], F32, name=f"shrunk{t}") for t in range(TILES - 1)]
-        shrunk_last = [table[1][:, U:], table[2][:, U:]]
-        fresh = {t: keep.tile([P, S], F32, name=f"fresh{t}") for t in range(TILES)}
+        shrunk = [keep.tile([P, S], F32, name=f"shrunk{t}") for t in range(TILES)]
+        early, late = slice(0, S - SHARE), slice(S - SHARE, S)
+        fresh = [keep.tile([P, S], F32, name=f"fresh{t}") for t in range(PAIR)]
+        fresh.append(shrunk[0])
 
-        for n in range(2):
-            for h in range(2):
-                nc.vector.tensor_scalar(step[n][:, :, halves[h]], bank[h][n][:], CLIP, -CLIP, ALU.min, ALU.max)
+        def step_of(n):
+            tiles, entries = groups[n]
+            return step[tiles[0] // PAIR][:, tiles[0] % PAIR : tiles[-1] % PAIR + 1, entries]
 
         def picked_of(t, entries):
             return table[t][:].indirect(ent_sb[:, list_columns(entries)])
 
+        def look_up(t, entries):
+            nc.scalar.activation(shrunk[t][:, entries], picked_of(t, entries), COPY, scale=DECAY)
+
+        def add(t, entries):
+            nc.gpsimd.tensor_tensor(fresh[t][:, entries], shrunk[t][:, entries], step[t // PAIR][:, t % PAIR, entries], ALU.add)
+
         def store(t):
-            nc.sync.dma_start(out=out_rows[:, t, :], in_=table[t][:, :U])
+            nc.sync.dma_start(out=out_rows[:, t, :], in_=table[t][:])
 
-        def add(t, entries, looked):
-            nc.gpsimd.tensor_tensor(fresh[t][:, entries], looked, step[t // PAIR][:, t % PAIR, entries], ALU.add)
+        for n in range(len(groups)):
+            nc.vector.tensor_scalar(step_of(n), bank[n][:], CLIP, -CLIP, ALU.min, ALU.max)
+        look_up(0, whole)
+        add(0, first)
+        add(0, slice(H, early.stop))
+        look_up(1, whole)
+        add(1, whole)
+        look_up(2, whole)
+        add(2, slice(0, SHARE))
+        fresh_late = shrunk[2][:, :SHARE]
+        nc.gpsimd.tensor_tensor(fresh_late, shrunk[0][:, late], step[0][:, 0, late], ALU.add)
+        add(2, slice(SHARE, S))
 
-        for t in range(TILES - 1):
-            nc.scalar.activation(shrunk[t][:], picked_of(t, whole), COPY, scale=DECAY)
-            for entries in halves if t == 0 else [whole]:
-                add(t, entries, shrunk[t][:, entries])
-        for h in range(2):
-            nc.scalar.activation(shrunk_last[h], picked_of(3, halves[h]), COPY, scale=DECAY)
-        first, second = halves
-        add(3, second, shrunk_last[1])
-
-        nc.vector.tensor_copy(picked_of(0, whole), fresh[0][:])
-        store(0)
+        nc.vector.tensor_copy(picked_of(0, early), fresh[0][:, early])
         nc.scalar.activation(picked_of(1, whole), fresh[1][:], COPY)
         store(1)
-        nc.vector.tensor_copy(picked_of(3, second), fresh[3][:, second])
-        nc.vector.tensor_tensor(picked_of(3, first), shrunk_last[0], step[1][:, 1, first], ALU.add)
+        nc.scalar.activation(picked_of(0, late), fresh_late, COPY)
+        store(0)
+        nc.vector.tensor_scalar(shrunk[3][:], picked_of(3, whole), DECAY, 0.0, ALU.mult, ALU.add)
+        nc.vector.tensor_tensor(picked_of(3, whole), shrunk[3][:], step[1][:, 1, :], ALU.add)
         store(3)
         nc.scalar.activation(picked_of(2, whole), fresh[2][:], COPY)
         store(2)

@@ -31,6 +31,7 @@ ALIGN = 256
 H = S // 2
 W_BYTES = PACK * N * 4
 SHARE = 96
+LEAD = 384
 X1_AT = PASSES * W_BYTES
 
 
@@ -148,10 +149,13 @@ def tile_picked_clipsgd_none_p_kernel(tc, x_words, x_scales, w1, par, offs, ent,
         products(1)
 
         step = [keep.tile([P, PAIR, S], F32, name=f"step{n}") for n in range(2)]
-        shrunk = [keep.tile([P, S], F32, name=f"shrunk{t}") for t in range(TILES)]
         early, late = slice(0, S - SHARE), slice(S - SHARE, S)
-        fresh = [keep.tile([P, S], F32, name=f"fresh{t}") for t in range(PAIR)]
-        fresh.append(shrunk[0])
+        lead, trail = slice(0, LEAD), slice(LEAD, S)
+        shrunk = [keep.tile([P, S], F32, name=f"shrunk{t}")[:] for t in range(TILES)]
+        fresh = [keep.tile([P, width], F32, name=f"fresh{t}")[:] for t, width in enumerate((early.stop, LEAD))]
+        fresh.append(shrunk[1])
+        fresh_late = shrunk[2][:, :SHARE]
+        fresh_trail = shrunk[0][:, trail]
 
         def step_of(n):
             tiles, entries = groups[n]
@@ -175,20 +179,21 @@ def tile_picked_clipsgd_none_p_kernel(tc, x_words, x_scales, w1, par, offs, ent,
         add(0, first)
         add(0, slice(H, early.stop))
         look_up(1, whole)
-        add(1, whole)
+        add(1, lead)
         look_up(2, whole)
         add(2, slice(0, SHARE))
-        fresh_late = shrunk[2][:, :SHARE]
         nc.gpsimd.tensor_tensor(fresh_late, shrunk[0][:, late], step[0][:, 0, late], ALU.add)
+        nc.gpsimd.tensor_tensor(fresh_trail, shrunk[1][:, trail], step[0][:, 1, trail], ALU.add)
         add(2, slice(SHARE, S))
 
-        nc.vector.tensor_copy(picked_of(0, early), fresh[0][:, early])
-        nc.scalar.activation(picked_of(1, whole), fresh[1][:], COPY)
-        store(1)
+        nc.vector.tensor_copy(picked_of(0, early), fresh[0])
+        nc.scalar.activation(picked_of(1, lead), fresh[1], COPY)
         nc.scalar.activation(picked_of(0, late), fresh_late, COPY)
         store(0)
-        nc.vector.tensor_scalar(shrunk[3][:], picked_of(3, whole), DECAY, 0.0, ALU.mult, ALU.add)
-        nc.vector.tensor_tensor(picked_of(3, whole), shrunk[3][:], step[1][:, 1, :], ALU.add)
+        nc.scalar.activation(picked_of(1, trail), fresh_trail, COPY)
+        store(1)
+        nc.vector.tensor_scalar(shrunk[3], picked_of(3, whole), DECAY, 0.0, ALU.mult, ALU.add)
+        nc.vector.tensor_tensor(picked_of(3, whole), shrunk[3], step[1][:, 1, :], ALU.add)
         store(3)
-        nc.scalar.activation(picked_of(2, whole), fresh[2][:], COPY)
+        nc.scalar.activation(picked_of(2, whole), fresh[2], COPY)
         store(2)

@@ -30,8 +30,7 @@ CLIP = 0.75
 ALIGN = 256
 H = S // 2
 W_BYTES = PACK * N * 4
-SHARE = 96
-LEAD = 384
+LATE = 128
 X1_AT = PASSES * W_BYTES
 
 
@@ -149,13 +148,13 @@ def tile_picked_clipsgd_none_p_kernel(tc, x_words, x_scales, w1, par, offs, ent,
         products(1)
 
         step = [keep.tile([P, PAIR, S], F32, name=f"step{n}") for n in range(2)]
-        early, late = slice(0, S - SHARE), slice(S - SHARE, S)
-        lead, trail = slice(0, LEAD), slice(LEAD, S)
-        shrunk = [keep.tile([P, S], F32, name=f"shrunk{t}")[:] for t in range(TILES)]
-        fresh = [keep.tile([P, width], F32, name=f"fresh{t}")[:] for t, width in enumerate((early.stop, LEAD))]
+        early, late = slice(0, S - LATE), slice(S - LATE, S)
+        shrunk_pair = keep.tile([P, PAIR, S], F32, name="shrunk_pair")
+        shrunk = [shrunk_pair[:, t, :] for t in range(PAIR)]
+        shrunk.extend(keep.tile([P, S], F32, name=f"shrunk{t}")[:] for t in range(PAIR, TILES))
+        fresh = [keep.tile([P, early.stop], F32, name=f"fresh{t}")[:] for t in range(PAIR)]
         fresh.append(shrunk[1])
-        fresh_late = shrunk[2][:, :SHARE]
-        fresh_trail = shrunk[0][:, trail]
+        fresh_late = shrunk[2][:, : PAIR * LATE].rearrange("p (t s) -> p t s", t=PAIR)
 
         def step_of(n):
             tiles, entries = groups[n]
@@ -179,19 +178,17 @@ def tile_picked_clipsgd_none_p_kernel(tc, x_words, x_scales, w1, par, offs, ent,
         add(0, first)
         add(0, slice(H, early.stop))
         look_up(1, whole)
-        add(1, lead)
+        add(1, early)
         look_up(2, whole)
-        add(2, slice(0, SHARE))
-        nc.gpsimd.tensor_tensor(fresh_late, shrunk[0][:, late], step[0][:, 0, late], ALU.add)
-        nc.gpsimd.tensor_tensor(fresh_trail, shrunk[1][:, trail], step[0][:, 1, trail], ALU.add)
-        add(2, slice(SHARE, S))
+        add(2, slice(0, PAIR * LATE))
+        nc.gpsimd.tensor_tensor(fresh_late, shrunk_pair[:, :, late], step[0][:, :, late], ALU.add)
+        add(2, slice(PAIR * LATE, S))
 
         nc.vector.tensor_copy(picked_of(0, early), fresh[0])
-        nc.scalar.activation(picked_of(1, lead), fresh[1], COPY)
-        nc.scalar.activation(picked_of(0, late), fresh_late, COPY)
-        store(0)
-        nc.scalar.activation(picked_of(1, trail), fresh_trail, COPY)
-        store(1)
+        nc.scalar.activation(picked_of(1, early), fresh[1], COPY)
+        for t in range(PAIR):
+            nc.scalar.activation(picked_of(t, late), fresh_late[:, t, :], COPY)
+            store(t)
         nc.vector.tensor_scalar(shrunk[3], picked_of(3, whole), DECAY, 0.0, ALU.mult, ALU.add)
         nc.vector.tensor_tensor(picked_of(3, whole), shrunk[3], step[1][:, 1, :], ALU.add)
         store(3)

from contextlib import ExitStack

import concourse.mybir as mybir

K, T, S, N, U = 1024, 2048, 512, 512, 1024
FLOPS = 2 * K * N * S

F32 = mybir.dt.float32
BF16 = mybir.dt.bfloat16
I32 = mybir.dt.int32
U32 = mybir.dt.uint32
U16 = mybir.dt.uint16
U8 = mybir.dt.uint8
FP8X4 = mybir.dt.float8_e4m3fn_x4
ALU = mybir.AluOpType
COPY = mybir.ActivationFunctionType.Copy

P = 128
PACK = 4
K_PASS = P * PACK
PASSES = K // K_PASS
TILES = N // P
PAIR = 2
QUAD = 32
QUAD_ROWS = 4
SPREAD = QUAD // QUAD_ROWS
GROUP = 16
DECAY = 0.875
CLIP = 0.75
ALIGN = 256
H = S // 2
W_BYTES = PACK * N * 4
LATE = 128
X1_AT = PASSES * W_BYTES


def tile_picked_clipsgd_none_p_kernel(tc, x_words, x_scales, w1, par, offs, ent, out):
    nc = tc.nc
    par_rows = par.rearrange("(p t) u -> p t u", t=TILES)
    out_rows = out.rearrange("(p t) u -> p t u", t=TILES)

    with ExitStack() as ctx:
        keep = ctx.enter_context(tc.tile_pool(name="keep", bufs=1))
        laid = ctx.enter_context(tc.tile_pool(name="laid", bufs=1))
        psum = ctx.enter_context(tc.psum_pool(name="psum", bufs=1))

        offs_sb = keep.tile([P, S // GROUP], U16, name="offs_sb", align_bytes=ALIGN)
        ent_sb = keep.tile([P, S // GROUP], U16, name="ent_sb", align_bytes=ALIGN)
        w_raw = [laid.tile([P, PACK, N], F32, name=f"w_raw{g}", align_bytes=ALIGN, offset=g * W_BYTES) for g in range(PASSES)]
        x_all = [keep.tile([P, T], U32, name="x_all0", align_bytes=ALIGN)]
        xs_all = keep.tile([P, T], U8, name="xs_all", align_bytes=ALIGN)

        def load_w(g):
            rows = w1[g * K_PASS : (g + 1) * K_PASS, :]
            nc.sync.dma_start(out=w_raw[g][:], in_=rows.rearrange("(p j) c -> p j c", j=PACK))

        def load_x(g):
            nc.sync.dma_start(out=x_all[g][:].bitcast(I32), in_=x_words[g].rearrange("p n r -> p (n r)").bitcast(I32))

        def list_columns(entries):
            return slice(entries.start // GROUP, entries.stop // GROUP)

        nc.vector.memset(xs_all[:].bitcast(I32), 0)

        load_x(0)
        for g in range(PASSES):
            nc.sync.dma_start(out=xs_all[QUAD_ROWS * g : P : SPREAD, :].bitcast(I32), in_=x_scales[g].bitcast(I32))
        nc.sync.dma_start(offs_sb[:], offs)
        load_w(0)
        load_w(1)
        nc.sync.dma_start(ent_sb[:], ent)

        x_scale = [keep.tile([P, S], U8, name=f"x_scale{g}", align_bytes=ALIGN) for g in range(PASSES)]
        w_bf = [keep.tile([P, TILES, P, PACK], BF16, name=f"w_bf{g}", align_bytes=ALIGN) for g in range(PASSES)]
        w_codes = [keep.tile([P, N], U32, name=f"w_codes{g}", align_bytes=ALIGN) for g in range(PASSES)]
        w_scales = [keep.tile([P, N], U8, name=f"w_scales{g}", align_bytes=ALIGN) for g in range(PASSES)]
        x_codes = [
            laid.tile([P, S], U32, name="x_codes0", align_bytes=ALIGN, offset=X1_AT + T * 4),
            keep.tile([P, S], U32, name="x_codes1", align_bytes=ALIGN),
        ]
        whole = slice(0, S)
        halves = [slice(0, H), slice(H, S)]
        tile_pairs = [slice(0, PAIR), slice(PAIR, TILES)]

        def cast_w(g):
            dst = w_bf[g][:].rearrange("p t m j -> p m j t")
            src = w_raw[g][:].rearrange("p j (m t) -> p m j t", t=TILES)
            early, late = tile_pairs
            nc.vector.tensor_scalar(dst[:, :, :, early], src[:, :, :, early], -1.0, None, ALU.mult)
            nc.scalar.activation(dst[:, :, :, late], src[:, :, :, late], COPY, scale=-1.0)

        def quantise_w(g):
            for pair in tile_pairs:
                features = slice(pair.start * P, pair.stop * P)
                nc.vector.quantize_mx(
                    out=w_codes[g][:, features].bitcast(FP8X4),
                    scales=w_scales[g][:, features],
                    in_=w_bf[g][:, pair].rearrange("p t m j -> p (t m j)"),
                )

        picked = laid.tile([P, S], U8, name="picked", align_bytes=ALIGN, offset=X1_AT + T * 4 - H)
        nc.vector.tensor_copy(picked[:], xs_all[:].indirect(offs_sb[:]))
        for g in range(PASSES):
            nc.vector.tensor_copy(x_scale[g][:].bitcast(I32), picked[:].bitcast(I32))

        def move_scale_rows(g):
            for i in range(1, QUAD_ROWS):
                nc.sync.dma_start(
                    out=x_scale[g][QUAD_ROWS * g + i : P : QUAD, :].bitcast(I32),
                    in_=x_scale[1 - g][QUAD_ROWS * g + SPREAD * i : P : QUAD, :].bitcast(I32),
                )

        move_scale_rows(0)
        x_all.append(laid.tile([P, T], U32, name="x_all1", align_bytes=ALIGN, offset=X1_AT))
        load_x(1)
        move_scale_rows(1)
        cast_w(0)
        quantise_w(0)
        nc.vector.tensor_copy(x_codes[0][:], x_all[0][:].indirect(offs_sb[:]))
        cast_w(1)
        quantise_w(1)

        table = [laid.tile([P, U], F32, name=f"table{t}", align_bytes=ALIGN, offset=t * U * 4) for t in range(TILES)]
        for t in range(TILES):
            nc.sync.dma_start(out=table[t][:], in_=par_rows[:, t, :])

        first, second = halves
        groups = [((0, 1), first), ((0, 1), second), ((2, 3), first), ((2, 3), second)]
        bank = [psum.tile([P, len(tiles), H], F32, name=f"bank{n}") for n, (tiles, entries) in enumerate(groups)]

        def products(g):
            for n, (tiles, entries) in enumerate(groups):
                for i, t in enumerate(tiles):
                    features = slice(t * P, (t + 1) * P)
                    nc.tensor.matmul_mx(
                        out=bank[n][:, i, :],
                        lhsT=w_codes[g][:, features].bitcast(FP8X4),
                        lhsT_scale=w_scales[g][:, features],
                        rhs=x_codes[g][:, entries].bitcast(FP8X4),
                        rhs_scale=x_scale[g][QUAD_ROWS * g : P, entries],
                        start=(g == 0 and i == 0),
                        stop=(g == PASSES - 1 and i == len(tiles) - 1),
                    )

        products(0)
        for entries in halves:
            nc.vector.tensor_copy(x_codes[1][:, entries], x_all[1][:].indirect(offs_sb[:, list_columns(entries)]))
        products(1)

        step = [keep.tile([P, PAIR, S], F32, name=f"step{n}") for n in range(2)]
        early, late = slice(0, S - LATE), slice(S - LATE, S)
        shrunk_pair = keep.tile([P, PAIR, S], F32, name="shrunk_pair")
        shrunk = [shrunk_pair[:, t, :] for t in range(PAIR)]
        shrunk.extend(keep.tile([P, S], F32, name=f"shrunk{t}")[:] for t in range(PAIR, TILES))
        fresh = [keep.tile([P, early.stop], F32, name=f"fresh{t}")[:] for t in range(PAIR)]
        fresh.append(shrunk[1])
        fresh_late = shrunk[2][:, : PAIR * LATE].rearrange("p (t s) -> p t s", t=PAIR)

        def step_of(n):
            tiles, entries = groups[n]
            return step[tiles[0] // PAIR][:, tiles[0] % PAIR : tiles[-1] % PAIR + 1, entries]

        def picked_of(t, entries):
            return table[t][:].indirect(ent_sb[:, list_columns(entries)])

        def look_up(t, entries):
            nc.scalar.activation(shrunk[t][:, entries], picked_of(t, entries), COPY, scale=DECAY)

        def add(t, entries):
            nc.gpsimd.tensor_tensor(fresh[t][:, entries], shrunk[t][:, entries], step[t // PAIR][:, t % PAIR, entries], ALU.add)

        def store(t):
            nc.sync.dma_start(out=out_rows[:, t, :], in_=table[t][:])

        for n in range(len(groups)):
            nc.vector.tensor_scalar(step_of(n), bank[n][:], CLIP, -CLIP, ALU.min, ALU.max)
        look_up(0, whole)
        add(0, first)
        add(0, slice(H, early.stop))
        look_up(1, whole)
        add(1, early)
        look_up(2, whole)
        add(2, slice(0, PAIR * LATE))
        nc.gpsimd.tensor_tensor(fresh_late, shrunk_pair[:, :, late], step[0][:, :, late], ALU.add)
        add(2, slice(PAIR * LATE, S))

        nc.vector.tensor_copy(picked_of(0, early), fresh[0])
        nc.scalar.activation(picked_of(1, early), fresh[1], COPY)
        for t in range(PAIR):
            nc.scalar.activation(picked_of(t, late), fresh_late[:, t, :], COPY)
            store(t)
        nc.vector.tensor_scalar(shrunk[3], picked_of(3, whole), DECAY, 0.0, ALU.mult, ALU.add)
        nc.vector.tensor_tensor(picked_of(3, whole), shrunk[3], step[1][:, 1, :], ALU.add)
        store(3)
        nc.scalar.activation(picked_of(2, whole), fresh[2], COPY)
        store(2)
